import numpy as np
import ml_dtypes


def mxq(x, axis, fmt="e4m3"):
    dtype, down = {"e4m3": (ml_dtypes.float8_e4m3fn, 7), "e5m2": (ml_dtypes.float8_e5m2, 14)}[fmt]
    v = np.moveaxis(np.asarray(x, np.float32).astype(ml_dtypes.bfloat16).astype(np.float64), axis, -1)
    blocks = v.reshape(v.shape[:-1] + (-1, 32))
    amax = np.abs(blocks).max(-1, keepdims=True)
    byte = np.maximum(np.where(amax > 0, np.frexp(amax)[1] - 1 + 127, 0) - down, 1)
    scale = np.exp2(byte - 127.0)
    codes = (blocks / scale).astype(np.float32).astype(dtype).astype(np.float64)
    return np.moveaxis((codes * scale).reshape(v.shape), -1, axis)


WIDE = False


def mx_kscale(k):
    if not WIDE:
        return np.ones(k)
    levels = np.array([10, -10, 5, -5, 0])
    if k % 512:
        return np.exp2(np.random.permutation(np.resize(levels, k // 32))).repeat(32)
    a = np.empty((k // 512, 16))
    for p in range(k // 512):
        a[p, :8] = np.random.permutation(np.resize(levels, 8))
        for g in range(8):
            far = levels[np.abs(levels - a[p, g]) >= 10]
            a[p, g + 8] = far[np.random.randint(len(far))]
    return np.exp2(a.ravel()).repeat(32)


def f64(x):
    return np.asarray(x).astype(np.float64)


def striped(idx):
    return np.tile(np.asarray(idx).reshape(-1, 16).T, (8, 1)).astype(np.uint16)


def unstriped(offs):
    return offs[:16].T.reshape(-1).astype(np.int64)


def sigmoid(v):
    return 1.0 / (1.0 + np.exp(-v))


def bf(x):
    return np.asarray(x, np.float32).astype(ml_dtypes.bfloat16)


def planes(Y):
    r, m = Y.shape
    b = f64(bf(Y)).reshape(r // 32, 32, m)
    amax = np.abs(b).max(1)
    byte = np.clip(np.where(amax > 0, np.frexp(amax)[1] - 1 + 127 - 7, 1), 1, 254)
    codes = (b * np.exp2(127.0 - byte)[:, None, :]).reshape(r, m).astype(np.float32).astype(ml_dtypes.float8_e4m3fn).view(np.uint8)
    words = codes.reshape(r // 512, 128, 4, m).transpose(0, 1, 3, 2)
    return np.ascontiguousarray(words), np.ascontiguousarray(byte.astype(np.uint8).reshape(r // 512, 16, m))


D, T, I, Q, E = 512, 1024, 512, 256, 512


def setup_inputs():
    n = np.random.standard_normal
    idx = np.random.permutation(T)[:I]
    fd = mx_kscale(D)
    fi = mx_kscale(I)
    ti = np.ones(T)
    ti[idx] = fi
    return {
        "query": (n((D, Q)) * 0.4 / np.sqrt(D) * fd[:, None]).astype(np.float32),
        "keys": (n((D, T)) / fd[:, None]).astype(np.float32),
        "kgate": (n((D, T))).astype(np.float32),
        "size": (np.random.uniform(0.5, 2.0, (1, I)) * fi).astype(np.float32),
        "vals": (n((E, T)) / ti).astype(np.float32),
        "offs": striped(idx),
    }


def reference(query, keys, kgate, size, vals, offs):
    idx = unstriped(offs)
    km = f64(keys)[:, idx] * sigmoid(f64(kgate)[:, idx])
    queryq = mxq(f64(query), 0, "e4m3")
    kmq = mxq(km, 0, "e4m3")
    a = queryq.T @ kmq
    p = np.exp(a - np.max(a, axis=1, keepdims=True))
    w = p * f64(size) / np.sum(p, axis=1, keepdims=True)
    wt = w.T
    vt = f64(vals)[:, idx].T
    vtq = mxq(vt, 0, "e4m3")
    wtq = mxq(wt, 0, "e4m3")
    o = vtq.T @ wtq
    words, scales = planes(o)
    return o, words, scales

@@ -1,0 +1,161 @@
+from contextlib import ExitStack
+
+import concourse.mybir as mybir
+from concourse.masks import make_identity
+
+F32 = mybir.dt.float32
+BF16 = mybir.dt.bfloat16
+I32 = mybir.dt.int32
+U32 = mybir.dt.uint32
+U16 = mybir.dt.uint16
+U8 = mybir.dt.uint8
+FP8X4 = mybir.dt.float8_e4m3fn_x4
+ACT = mybir.ActivationFunctionType
+ALU = mybir.AluOpType
+AX = mybir.AxisListType
+
+D, T, I, Q, E = 512, 1024, 512, 256, 512
+P = 128
+PACK = 4
+HALF = I // 2
+FLOPS = 2 * D * Q * I + 2 * I * E * Q
+
+
+def tile_attend_gatedkeys_pl_kernel(tc, query, keys, kgate, size, vals, offs, out_0, out_1, out_2):
+    nc = tc.nc
+    with ExitStack() as ctx:
+        sb = ctx.enter_context(tc.tile_pool(name="sb", bufs=1))
+        ps = ctx.enter_context(tc.psum_pool(name="ps", bufs=1))
+
+        def sbuf(name, shape, dtype):
+            return sb.tile(shape, dtype, name=name, align_bytes=64)
+
+        def bank(name, tag=None):
+            return ps.tile([P, 512], F32, name=name, tag=tag or name)
+
+        def weave(copy, dst, src):
+            copy(out=dst.rearrange("p (c i) t -> p c t i", i=4), in_=src.rearrange("p t (c i) -> p c t i", i=4))
+
+        def quantize(codes, scales, src):
+            nc.vector.quantize_mx(out=codes.bitcast(FP8X4), scales=scales, in_=src.rearrange("p c t -> p (c t)"))
+
+        offsets = sbuf("offsets", [P, I // 16], U16)
+        nc.sync.dma_start(offsets[:], offs)
+        gate_rows = kgate.rearrange("(p t) n -> p t n", t=PACK)
+        key_rows = keys.rearrange("(p t) n -> p t n", t=PACK)
+        val_rows = vals.rearrange("(p t) n -> p t n", t=PACK)
+        gate_pool = [sbuf(f"gate_pool{t}", [P, T], F32) for t in range(PACK)]
+        key_pool = [sbuf(f"key_pool{t}", [P, T], F32) for t in range(PACK)]
+        val_pool = [sbuf(f"val_pool{t}", [P, T], F32) for t in range(PACK)]
+        query_raw = sbuf("query_raw", [P, PACK, Q], F32)
+        size_cols = sbuf("size_cols", [P, PACK], F32)
+        srcs = {"g": (gate_pool, gate_rows), "k": (key_pool, key_rows), "v": (val_pool, val_rows)}
+        for item in "g0 k0 g1 k1 g2 k2 g3 k3 q s v0 v1 v2 v3".split():
+            if item == "q":
+                nc.sync.dma_start(query_raw[:], query.rearrange("(p t) q -> p t q", t=PACK))
+            elif item == "s":
+                nc.sync.dma_start(size_cols[:], size.rearrange("o (p t) -> p (o t)", t=PACK))
+            else:
+                pool_tiles, rows = srcs[item[0]]
+                nc.sync.dma_start(pool_tiles[int(item[1])][:], rows[:, int(item[1]), :])
+
+        ident = sbuf("ident", [P, P], F32)
+        make_identity(nc, ident[:])
+
+        gates = [[sbuf(f"gate{t}_{h}", [P, HALF], F32) for h in range(2)] for t in range(PACK)]
+        km = [sbuf(f"km{h}", [P, PACK, HALF], F32) for h in range(2)]
+        for t in range(PACK):
+            for h in range(2):
+                lst = offsets[:, 16 * h : 16 * (h + 1)]
+                nc.scalar.activation(gates[t][h][:], gate_pool[t][:].indirect(lst), ACT.Sigmoid)
+            for h in range(2):
+                lst = offsets[:, 16 * h : 16 * (h + 1)]
+                nc.vector.tensor_tensor(km[h][:, t, :], key_pool[t][:].indirect(lst), gates[t][h][:], ALU.mult)
+
+        km_bf = [sbuf(f"km_bf{h}", [P, HALF, PACK], BF16) for h in range(2)]
+        k_codes = sbuf("k_codes", [P, I], U32)
+        k_scales = sbuf("k_scales", [P, I], U8)
+        q_bf = [sbuf(f"q_bf{b}", [P, P, PACK], BF16) for b in range(2)]
+        q_codes = [sbuf(f"q_codes{b}", [P, P], U32) for b in range(2)]
+        q_scales = [sbuf(f"q_scales{b}", [P, P], U8) for b in range(2)]
+        weave(nc.scalar.copy, km_bf[0][:], km[0][:])
+        weave(nc.vector.tensor_copy, km_bf[1][:], km[1][:])
+        weave(nc.scalar.copy, q_bf[0][:], query_raw[:, :, 0:P])
+        weave(nc.scalar.copy, q_bf[1][:], query_raw[:, :, P:Q])
+        quantize(k_codes[:, HALF:I], k_scales[:, HALF:I], km_bf[1][:])
+        quantize(k_codes[:, 0:HALF], k_scales[:, 0:HALF], km_bf[0][:])
+        quantize(q_codes[0][:], q_scales[0][:], q_bf[0][:])
+        quantize(q_codes[1][:], q_scales[1][:], q_bf[1][:])
+
+        size_bank = bank("size_bank")
+        for t in range(PACK):
+            nc.tensor.transpose(size_bank[:, t * P : (t + 1) * P], size_cols[:, t : t + 1].to_broadcast([P, P]), ident[:])
+
+        scores = [bank(f"scores{b}") for b in range(2)]
+        for b in range(2):
+            nc.tensor.matmul_mx(out=scores[b][:], lhsT=q_codes[b][:].bitcast(FP8X4), lhsT_scale=q_scales[b][:],
+                                rhs=k_codes[:].bitcast(FP8X4), rhs_scale=k_scales[:], start=True, stop=True)
+
+        def turn(src_bf, turned, name):
+            words = src_bf[:].bitcast(F32)
+            for u in range(2):
+                nc.tensor.transpose(turned[:, u * P : (u + 1) * P], words[:, u : 2 * P : 2], ident[:])
+            woven = sbuf(name + "_bf", [P, P, PACK], BF16)
+            nc.scalar.copy(out=woven[:].rearrange("p c t -> p (c t)").bitcast(F32).rearrange("p (c u) -> p c u", u=2),
+                           in_=turned[:, 0 : 2 * P].rearrange("p (u c) -> p c u", u=2))
+            codes = sbuf(name + "_codes", [P, P], U32)
+            scales = sbuf(name + "_scales", [P, P], U8)
+            quantize(codes[:], scales[:], woven[:])
+            return codes, scales
+
+        def values(t):
+            picked = sbuf(f"v_picked{t}", [P, I], BF16)
+            nc.vector.tensor_copy(picked[:], val_pool[t][:].indirect(offsets[:]))
+            return turn(picked, bank(f"v_turned{t}", tag=f"vt{t % 3}"), f"v{t}")
+
+        neg_max = [sbuf(f"neg_max{b}", [P, 1], F32) for b in range(2)]
+        sums = [sbuf(f"sums{b}", [P, 1], F32) for b in range(2)]
+        inv = [sbuf(f"inv{b}", [P, 1], F32) for b in range(2)]
+        probs = [sbuf(f"probs{b}", [P, I], F32) for b in range(2)]
+        w_bf = [sbuf(f"w_bf{b}", [P, I], BF16) for b in range(2)]
+
+        def softmax_max(b):
+            nc.vector.tensor_reduce(neg_max[b][:], scores[b][:], AX.X, ALU.max, negate=True)
+            nc.scalar.activation(probs[b][:], scores[b][:], ACT.Exp, bias=neg_max[b][:], accum_out=sums[b][:])
+
+        def weights(b):
+            nc.vector.reciprocal(inv[b][:], sums[b][:])
+            nc.vector.scalar_tensor_tensor(
+                w_bf[b][:].rearrange("p (s t) -> p s t", t=PACK), probs[b][:].rearrange("p (s t) -> p s t", t=PACK),
+                inv[b][:], size_bank[:].rearrange("p (t s) -> p s t", t=PACK), ALU.mult, ALU.mult)
+            return turn(w_bf[b], bank(f"w_turned{b}", tag=f"scores{b}"), f"w{b}")
+
+        v_ops = [values(0)]
+        softmax_max(0)
+        softmax_max(1)
+        v_ops.append(values(1))
+        w_ops = [weights(0)]
+        v_ops.append(values(2))
+        v_ops.append(values(3))
+        w_ops.append(weights(1))
+
+        o_codes = sbuf("o_codes", [P, Q], U32)
+        o_scales = sbuf("o_scales", [P, Q], U8)
+        out_rows = out_0.rearrange("(p t) q -> p t q", t=PACK)
+        out_words = out_1.rearrange("z p c r -> p (z c r)").bitcast(I32)
+        for b in range(2):
+            cols = slice(b * P, (b + 1) * P)
+            acc = bank(f"acc{b}")
+            for t in range(PACK):
+                nc.tensor.matmul_mx(out=acc[:, t * P : (t + 1) * P], lhsT=v_ops[t][0][:].bitcast(FP8X4), lhsT_scale=v_ops[t][1][:],
+                                    rhs=w_ops[b][0][:].bitcast(FP8X4), rhs_scale=w_ops[b][1][:], start=True, stop=True)
+            result_bf = sbuf(f"result_bf{b}", [P, P, PACK], BF16)
+            nc.vector.tensor_copy(out=result_bf[:], in_=acc[:].rearrange("p (t q) -> p q t", t=PACK))
+            result = sbuf(f"result{b}", [P, PACK, P], F32)
+            nc.scalar.copy(out=result[:].rearrange("p t q -> p (t q)"), in_=acc[:])
+            nc.sync.dma_start(out_rows[:, :, cols], result[:])
+            quantize(o_codes[:, cols], o_scales[:, cols], result_bf[:])
+            nc.sync.dma_start(out_words[:, cols], o_codes[:, cols].bitcast(I32))
+        for g in range(4):
+            queue = nc.sync if g % 2 == 0 else nc.scalar
+            queue.dma_start(out_2[0, 4 * g : 4 * g + 4, :].bitcast(I32), o_scales[32 * g : 32 * g + 4, :].bitcast(I32))

@@ -27,8 +27,8 @@ def tile_attend_gatedkeys_pl_kernel(tc, query, keys, kgate, size, vals, offs, ou
         sb = ctx.enter_context(tc.tile_pool(name="sb", bufs=1))
         ps = ctx.enter_context(tc.psum_pool(name="ps", bufs=1))
 
-        def sbuf(name, shape, dtype):
-            return sb.tile(shape, dtype, name=name, align_bytes=64)
+        def sbuf(name, shape, dtype, tag=None):
+            return sb.tile(shape, dtype, name=name, tag=tag or name, align_bytes=64)
 
         def bank(name, tag=None):
             return ps.tile([P, 512], F32, name=name, tag=tag or name)
@@ -50,7 +50,7 @@ def tile_attend_gatedkeys_pl_kernel(tc, query, keys, kgate, size, vals, offs, ou
         query_raw = sbuf("query_raw", [P, PACK, Q], F32)
         size_cols = sbuf("size_cols", [P, PACK], F32)
         srcs = {"g": (gate_pool, gate_rows), "k": (key_pool, key_rows), "v": (val_pool, val_rows)}
-        for item in "g0 k0 g1 k1 g2 k2 g3 k3 q s v0 v1 v2 v3".split():
+        for item in "g0 k0 g1 k1 g2 g3 k2 k3 q s v0 v1 v2 v3".split():
             if item == "q":
                 nc.sync.dma_start(query_raw[:], query.rearrange("(p t) q -> p t q", t=PACK))
             elif item == "s":
@@ -62,6 +62,34 @@ def tile_attend_gatedkeys_pl_kernel(tc, query, keys, kgate, size, vals, offs, ou
         ident = sbuf("ident", [P, P], F32)
         make_identity(nc, ident[:])
 
+        def turn(word_halves, turned, name):
+            for u in range(2):
+                nc.tensor.transpose(turned[:, u * P : (u + 1) * P], word_halves[u], ident[:])
+            woven = sbuf(name + "_bf", [P, P, PACK], BF16)
+            nc.scalar.copy(out=woven[:].rearrange("p c t -> p (c t)").bitcast(F32).rearrange("p (c u) -> p c u", u=2),
+                           in_=turned[:, 0 : 2 * P].rearrange("p (u c) -> p c u", u=2))
+            codes = sbuf(name + "_codes", [P, P], U32)
+            scales = sbuf(name + "_scales", [P, P], U8)
+            quantize(codes[:], scales[:], woven[:])
+            return codes, scales
+
+        def pick(t):
+            picked = sbuf(f"v_picked{t}", [P, I], BF16, {}.get(t))
+            if t in (0, 2):
+                narrow = sbuf(f"val_narrow{t}", [P, T], BF16, {}.get(t))
+                if t in (2,):
+                    nc.vector.tensor_copy(narrow[:], val_pool[t][:])
+                else:
+                    nc.scalar.activation(narrow[:], val_pool[t][:], ACT.Copy)
+                nc.scalar.activation(picked[:], narrow[:].indirect(offsets[:]), ACT.Copy)
+            else:
+                nc.vector.tensor_copy(picked[:], val_pool[t][:].indirect(offsets[:]))
+            return picked
+
+        def values(t, picked):
+            words = picked[:].bitcast(F32)
+            return turn([words[:, u : 2 * P : 2] for u in range(2)], bank(f"v_turned{t}", tag=f"vt{t % 3}"), f"v{t}")
+
         gates = [[sbuf(f"gate{t}_{h}", [P, HALF], F32) for h in range(2)] for t in range(PACK)]
         km = [sbuf(f"km{h}", [P, PACK, HALF], F32) for h in range(2)]
         for t in range(PACK):
@@ -71,89 +99,79 @@ def tile_attend_gatedkeys_pl_kernel(tc, query, keys, kgate, size, vals, offs, ou
             for h in range(2):
                 lst = offsets[:, 16 * h : 16 * (h + 1)]
                 nc.vector.tensor_tensor(km[h][:, t, :], key_pool[t][:].indirect(lst), gates[t][h][:], ALU.mult)
-
-        km_bf = [sbuf(f"km_bf{h}", [P, HALF, PACK], BF16) for h in range(2)]
-        k_codes = sbuf("k_codes", [P, I], U32)
-        k_scales = sbuf("k_scales", [P, I], U8)
-        q_bf = [sbuf(f"q_bf{b}", [P, P, PACK], BF16) for b in range(2)]
-        q_codes = [sbuf(f"q_codes{b}", [P, P], U32) for b in range(2)]
-        q_scales = [sbuf(f"q_scales{b}", [P, P], U8) for b in range(2)]
-        weave(nc.scalar.copy, km_bf[0][:], km[0][:])
-        weave(nc.vector.tensor_copy, km_bf[1][:], km[1][:])
-        weave(nc.scalar.copy, q_bf[0][:], query_raw[:, :, 0:P])
-        weave(nc.scalar.copy, q_bf[1][:], query_raw[:, :, P:Q])
-        quantize(k_codes[:, HALF:I], k_scales[:, HALF:I], km_bf[1][:])
-        quantize(k_codes[:, 0:HALF], k_scales[:, 0:HALF], km_bf[0][:])
-        quantize(q_codes[0][:], q_scales[0][:], q_bf[0][:])
-        quantize(q_codes[1][:], q_scales[1][:], q_bf[1][:])
+        warm2 = sbuf("warm2", [P, 1], F32)
+        nc.scalar.activation(warm2[:], gates[3][1][:, 0:1], ACT.Exp)
 
         size_bank = bank("size_bank")
         for t in range(PACK):
             nc.tensor.transpose(size_bank[:, t * P : (t + 1) * P], size_cols[:, t : t + 1].to_broadcast([P, P]), ident[:])
+        size_dealt = size_bank[:].rearrange("p (u r s) -> p u s r", u=2, r=2)
+
+        km_bf = [sbuf(f"km_bf{h}", [P, HALF, PACK], BF16) for h in range(2)]
+        k_codes = [sbuf(f"k_codes{h}", [P, HALF], U32) for h in range(2)]
+        k_scales = [sbuf(f"k_scales{h}", [P, HALF], U8) for h in range(2)]
+        q_bf = [sbuf(f"q_bf{b}", [P, P, PACK], BF16) for b in range(2)]
+        q_codes = [sbuf(f"q_codes{b}", [P, P], U32) for b in range(2)]
+        q_scales = [sbuf(f"q_scales{b}", [P, P], U8) for b in range(2)]
+        weave(nc.scalar.copy, km_bf[0][:], km[0][:])
+        weave(nc.vector.tensor_copy, q_bf[0][:], query_raw[:, :, 0:P])
+        weave(nc.vector.tensor_copy, km_bf[1][:], km[1][:])
+        weave(nc.scalar.copy, q_bf[1][:], query_raw[:, :, P:Q])
+        quantize(q_codes[0][:], q_scales[0][:], q_bf[0][:])
+        quantize(k_codes[0][:], k_scales[0][:], km_bf[0][:])
+        quantize(k_codes[1][:], k_scales[1][:], km_bf[1][:])
+        quantize(q_codes[1][:], q_scales[1][:], q_bf[1][:])
 
         scores = [bank(f"scores{b}") for b in range(2)]
         for b in range(2):
-            nc.tensor.matmul_mx(out=scores[b][:], lhsT=q_codes[b][:].bitcast(FP8X4), lhsT_scale=q_scales[b][:],
-                                rhs=k_codes[:].bitcast(FP8X4), rhs_scale=k_scales[:], start=True, stop=True)
+            for h in range(2):
+                nc.tensor.matmul_mx(out=scores[b][:, h * HALF : (h + 1) * HALF], lhsT=q_codes[b][:].bitcast(FP8X4), lhsT_scale=q_scales[b][:],
+                                    rhs=k_codes[h][:].bitcast(FP8X4), rhs_scale=k_scales[h][:], start=True, stop=True)
 
-        def turn(src_bf, turned, name):
-            words = src_bf[:].bitcast(F32)
-            for u in range(2):
-                nc.tensor.transpose(turned[:, u * P : (u + 1) * P], words[:, u : 2 * P : 2], ident[:])
-            woven = sbuf(name + "_bf", [P, P, PACK], BF16)
-            nc.scalar.copy(out=woven[:].rearrange("p c t -> p (c t)").bitcast(F32).rearrange("p (c u) -> p c u", u=2),
-                           in_=turned[:, 0 : 2 * P].rearrange("p (u c) -> p c u", u=2))
-            codes = sbuf(name + "_codes", [P, P], U32)
-            scales = sbuf(name + "_scales", [P, P], U8)
-            quantize(codes[:], scales[:], woven[:])
-            return codes, scales
-
-        def values(t):
-            picked = sbuf(f"v_picked{t}", [P, I], BF16)
-            nc.vector.tensor_copy(picked[:], val_pool[t][:].indirect(offsets[:]))
-            return turn(picked, bank(f"v_turned{t}", tag=f"vt{t % 3}"), f"v{t}")
-
-        neg_max = [sbuf(f"neg_max{b}", [P, 1], F32) for b in range(2)]
+        picked = {t: pick(t) for t in (1,)}
+        neg_max = sbuf("neg_max", [P, 2], F32, "val_pool1")
         sums = [sbuf(f"sums{b}", [P, 1], F32) for b in range(2)]
-        inv = [sbuf(f"inv{b}", [P, 1], F32) for b in range(2)]
-        probs = [sbuf(f"probs{b}", [P, I], F32) for b in range(2)]
-        w_bf = [sbuf(f"w_bf{b}", [P, I], BF16) for b in range(2)]
+        inv = [sbuf(f"inv{b}", [P, 1], F32, (None, None)[b]) for b in range(2)]
+        probs = [sbuf(f"probs{b}", [P, 2, P, 2], F32) for b in range(2)]
+        for b in range(2):
+            nc.vector.tensor_reduce(neg_max[:, b : b + 1], scores[b][:], AX.X, ALU.max, negate=True)
+            nc.scalar.activation(probs[b][:], scores[b][:].rearrange("p (s u r) -> p u s r", u=2, r=2), ACT.Exp,
+                                 bias=neg_max[:, b : b + 1], accum_out=sums[b][:])
+        for t in ():
+            picked[t] = pick(t)
 
-        def softmax_max(b):
-            nc.vector.tensor_reduce(neg_max[b][:], scores[b][:], AX.X, ALU.max, negate=True)
-            nc.scalar.activation(probs[b][:], scores[b][:], ACT.Exp, bias=neg_max[b][:], accum_out=sums[b][:])
-
-        def weights(b):
+        w_bf = [[sbuf(f"w_bf{b}_{u}", [P, P, 2], BF16, {}.get((b, u))) for u in range(2)] for b in range(2)]
+        for b in range(2):
             nc.vector.reciprocal(inv[b][:], sums[b][:])
-            nc.vector.scalar_tensor_tensor(
-                w_bf[b][:].rearrange("p (s t) -> p s t", t=PACK), probs[b][:].rearrange("p (s t) -> p s t", t=PACK),
-                inv[b][:], size_bank[:].rearrange("p (t s) -> p s t", t=PACK), ALU.mult, ALU.mult)
-            return turn(w_bf[b], bank(f"w_turned{b}", tag=f"scores{b}"), f"w{b}")
-
-        v_ops = [values(0)]
-        softmax_max(0)
-        softmax_max(1)
-        v_ops.append(values(1))
-        w_ops = [weights(0)]
-        v_ops.append(values(2))
-        v_ops.append(values(3))
-        w_ops.append(weights(1))
+            for u in range(2):
+                nc.vector.scalar_tensor_tensor(w_bf[b][u][:], probs[b][:, u], inv[b][:], size_dealt[:, u], ALU.mult, ALU.mult)
+        w_ops = [
+            turn([w_bf[b][u][:].rearrange("p s r -> p (s r)").bitcast(F32) for u in range(2)], bank(f"w_turned{b}", tag=f"scores{b}"), f"w{b}")
+            for b in range(2)
+        ]
+        for t in (0, 2, 3):
+            picked[t] = pick(t)
+        v_ops = [values(t, picked[t]) for t in range(PACK)]
 
         o_codes = sbuf("o_codes", [P, Q], U32)
         o_scales = sbuf("o_scales", [P, Q], U8)
         out_rows = out_0.rearrange("(p t) q -> p t q", t=PACK)
         out_words = out_1.rearrange("z p c r -> p (z c r)").bitcast(I32)
+        acc_tags = [["acc_x", "acc_y"], ["scores0", "size_bank"]]
         for b in range(2):
             cols = slice(b * P, (b + 1) * P)
-            acc = bank(f"acc{b}")
-            for t in range(PACK):
-                nc.tensor.matmul_mx(out=acc[:, t * P : (t + 1) * P], lhsT=v_ops[t][0][:].bitcast(FP8X4), lhsT_scale=v_ops[t][1][:],
-                                    rhs=w_ops[b][0][:].bitcast(FP8X4), rhs_scale=w_ops[b][1][:], start=True, stop=True)
-            result_bf = sbuf(f"result_bf{b}", [P, P, PACK], BF16)
-            nc.vector.tensor_copy(out=result_bf[:], in_=acc[:].rearrange("p (t q) -> p q t", t=PACK))
             result = sbuf(f"result{b}", [P, PACK, P], F32)
-            nc.scalar.copy(out=result[:].rearrange("p t q -> p (t q)"), in_=acc[:])
-            nc.sync.dma_start(out_rows[:, :, cols], result[:])
+            for pair in range(2):
+                acc = bank(f"acc{b}_{pair}", tag=acc_tags[b][pair])
+                for r in range(2):
+                    t = 2 * pair + r
+                    nc.tensor.matmul_mx(out=acc[:, r * P : (r + 1) * P], lhsT=v_ops[t][0][:].bitcast(FP8X4), lhsT_scale=v_ops[t][1][:],
+                                        rhs=w_ops[b][0][:].bitcast(FP8X4), rhs_scale=w_ops[b][1][:], start=True, stop=True)
+                rows = slice(2 * pair, 2 * pair + 2)
+                nc.scalar.copy(out=result[:, rows, :].rearrange("p t q -> p (t q)"), in_=acc[:, 0 : 2 * P])
+                nc.sync.dma_start(out_rows[:, rows, cols], result[:, rows, :])
+            result_bf = sbuf(f"result_bf{b}", [P, P, PACK], BF16)
+            weave(nc.vector.tensor_copy, result_bf[:], result[:])
             quantize(o_codes[:, cols], o_scales[:, cols], result_bf[:])
             nc.sync.dma_start(out_words[:, cols], o_codes[:, cols].bitcast(I32))
         for g in range(4):

@@ -18,6 +18,8 @@ D, T, I, Q, E = 512, 1024, 512, 256, 512
 P = 128
 PACK = 4
 HALF = I // 2
+QUARTER = I // 4
+LIST_ROWS = 16
 FLOPS = 2 * D * Q * I + 2 * I * E * Q
 
 
@@ -27,153 +29,192 @@ def tile_attend_gatedkeys_pl_kernel(tc, query, keys, kgate, size, vals, offs, ou
         sb = ctx.enter_context(tc.tile_pool(name="sb", bufs=1))
         ps = ctx.enter_context(tc.psum_pool(name="ps", bufs=1))
 
-        def sbuf(name, shape, dtype, tag=None):
-            return sb.tile(shape, dtype, name=name, tag=tag or name, align_bytes=64)
+        def sbuf(name, shape, dtype, bytes_of=None):
+            return sb.tile(shape, dtype, name=name, tag=bytes_of or name, align_bytes=64)
 
-        def bank(name, tag=None):
-            return ps.tile([P, 512], F32, name=name, tag=tag or name)
+        def bank(name, bytes_of=None):
+            return ps.tile([P, 512], F32, name=name, tag=bytes_of or name)
 
         def weave(copy, dst, src):
             copy(out=dst.rearrange("p (c i) t -> p c t i", i=4), in_=src.rearrange("p t (c i) -> p c t i", i=4))
 
-        def quantize(codes, scales, src):
-            nc.vector.quantize_mx(out=codes.bitcast(FP8X4), scales=scales, in_=src.rearrange("p c t -> p (c t)"))
+        def quantize(codes, scales, woven):
+            nc.vector.quantize_mx(out=codes.bitcast(FP8X4), scales=scales, in_=woven.rearrange("p c t -> p (c t)"))
 
-        offsets = sbuf("offsets", [P, I // 16], U16)
+        def product(out, stationary, moving):
+            nc.tensor.matmul_mx(out=out, lhsT=stationary[0].bitcast(FP8X4), lhsT_scale=stationary[1],
+                                rhs=moving[0].bitcast(FP8X4), rhs_scale=moving[1], start=True, stop=True)
+
+        offsets = sbuf("offsets", [P, I // LIST_ROWS], U16)
         nc.sync.dma_start(offsets[:], offs)
-        gate_rows = kgate.rearrange("(p t) n -> p t n", t=PACK)
-        key_rows = keys.rearrange("(p t) n -> p t n", t=PACK)
-        val_rows = vals.rearrange("(p t) n -> p t n", t=PACK)
         gate_pool = [sbuf(f"gate_pool{t}", [P, T], F32) for t in range(PACK)]
         key_pool = [sbuf(f"key_pool{t}", [P, T], F32) for t in range(PACK)]
         val_pool = [sbuf(f"val_pool{t}", [P, T], F32) for t in range(PACK)]
         query_raw = sbuf("query_raw", [P, PACK, Q], F32)
         size_cols = sbuf("size_cols", [P, PACK], F32)
-        srcs = {"g": (gate_pool, gate_rows), "k": (key_pool, key_rows), "v": (val_pool, val_rows)}
-        for item in "g0 k0 g1 k1 g2 g3 k2 k3 q s v0 v1 v2 v3".split():
-            if item == "q":
-                nc.sync.dma_start(query_raw[:], query.rearrange("(p t) q -> p t q", t=PACK))
-            elif item == "s":
-                nc.sync.dma_start(size_cols[:], size.rearrange("o (p t) -> p (o t)", t=PACK))
-            else:
-                pool_tiles, rows = srcs[item[0]]
-                nc.sync.dma_start(pool_tiles[int(item[1])][:], rows[:, int(item[1]), :])
+
+        def load_plane(pool, source, t):
+            nc.sync.dma_start(pool[t][:], source.rearrange("(p t) n -> p t n", t=PACK)[:, t, :])
+
+        for t in range(2):
+            load_plane(gate_pool, kgate, t)
+            load_plane(key_pool, keys, t)
+        for pool, source in ((gate_pool, kgate), (key_pool, keys)):
+            for t in range(2, PACK):
+                load_plane(pool, source, t)
+        nc.sync.dma_start(query_raw[:], query.rearrange("(p t) q -> p t q", t=PACK))
+        for t in range(PACK - 1):
+            load_plane(val_pool, vals, t)
+        nc.sync.dma_start(size_cols[:], size.rearrange("o (p t) -> p (o t)", t=PACK))
+        load_plane(val_pool, vals, PACK - 1)
 
         ident = sbuf("ident", [P, P], F32)
         make_identity(nc, ident[:])
 
-        def turn(word_halves, turned, name):
-            for u in range(2):
-                nc.tensor.transpose(turned[:, u * P : (u + 1) * P], word_halves[u], ident[:])
-            woven = sbuf(name + "_bf", [P, P, PACK], BF16)
-            nc.scalar.copy(out=woven[:].rearrange("p c t -> p (c t)").bitcast(F32).rearrange("p (c u) -> p c u", u=2),
-                           in_=turned[:, 0 : 2 * P].rearrange("p (u c) -> p c u", u=2))
-            codes = sbuf(name + "_codes", [P, P], U32)
-            scales = sbuf(name + "_scales", [P, P], U8)
-            quantize(codes[:], scales[:], woven[:])
-            return codes, scales
-
-        def pick(t):
-            picked = sbuf(f"v_picked{t}", [P, I], BF16, {}.get(t))
-            if t in (0, 2):
-                narrow = sbuf(f"val_narrow{t}", [P, T], BF16, {}.get(t))
-                if t in (2,):
-                    nc.vector.tensor_copy(narrow[:], val_pool[t][:])
-                else:
-                    nc.scalar.activation(narrow[:], val_pool[t][:], ACT.Copy)
-                nc.scalar.activation(picked[:], narrow[:].indirect(offsets[:]), ACT.Copy)
-            else:
-                nc.vector.tensor_copy(picked[:], val_pool[t][:].indirect(offsets[:]))
-            return picked
-
-        def values(t, picked):
-            words = picked[:].bitcast(F32)
-            return turn([words[:, u : 2 * P : 2] for u in range(2)], bank(f"v_turned{t}", tag=f"vt{t % 3}"), f"v{t}")
+        def listed(pool_tile, start, stop):
+            return pool_tile[:].indirect(offsets[:, start // LIST_ROWS : stop // LIST_ROWS])
 
         gates = [[sbuf(f"gate{t}_{h}", [P, HALF], F32) for h in range(2)] for t in range(PACK)]
         km = [sbuf(f"km{h}", [P, PACK, HALF], F32) for h in range(2)]
         for t in range(PACK):
             for h in range(2):
-                lst = offsets[:, 16 * h : 16 * (h + 1)]
-                nc.scalar.activation(gates[t][h][:], gate_pool[t][:].indirect(lst), ACT.Sigmoid)
+                nc.scalar.activation(gates[t][h][:], listed(gate_pool[t], h * HALF, (h + 1) * HALF), ACT.Sigmoid)
             for h in range(2):
-                lst = offsets[:, 16 * h : 16 * (h + 1)]
-                nc.vector.tensor_tensor(km[h][:, t, :], key_pool[t][:].indirect(lst), gates[t][h][:], ALU.mult)
-        warm2 = sbuf("warm2", [P, 1], F32)
-        nc.scalar.activation(warm2[:], gates[3][1][:, 0:1], ACT.Exp)
+                nc.vector.tensor_tensor(km[h][:, t, :], listed(key_pool[t], h * HALF, (h + 1) * HALF), gates[t][h][:], ALU.mult)
+        exp_warm = sbuf("exp_warm", [P, 1], F32)
+        nc.scalar.activation(exp_warm[:], gates[PACK - 1][0][:, 0:1], ACT.Exp)
+
+        q_bf = [sbuf(f"q_bf{b}", [P, P, PACK], BF16) for b in range(2)]
+        km_bf = [sbuf("km_bf0", [P, HALF, PACK], BF16)]
+        for b in range(2):
+            weave(nc.scalar.copy, q_bf[b][:], query_raw[:, :, b * P : (b + 1) * P])
+        for c in range(2):
+            weave(nc.vector.tensor_copy, km_bf[0][:, c * QUARTER : (c + 1) * QUARTER, :], km[0][:, :, c * QUARTER : (c + 1) * QUARTER])
+        km_bf.append(sbuf("km_bf1", [P, HALF, PACK], BF16, "query_raw"))
+        weave(nc.scalar.copy, km_bf[1][:], km[1][:])
+
+        k_mx = [(sbuf(f"k_codes{h}", [P, HALF], U32)[:], sbuf(f"k_scales{h}", [P, HALF], U8)[:]) for h in range(2)]
+        q_mx = [(sbuf(f"q_codes{b}", [P, P], U32)[:], sbuf(f"q_scales{b}", [P, P], U8)[:]) for b in range(2)]
+        quantize(*q_mx[0], q_bf[0][:])
+        for c in range(2):
+            cols = slice(c * QUARTER, (c + 1) * QUARTER)
+            quantize(k_mx[0][0][:, cols], k_mx[0][1][:, cols], km_bf[0][:, cols, :])
+        quantize(*q_mx[1], q_bf[1][:])
+        quantize(*k_mx[1], km_bf[1][:])
+
+        scores = [bank(f"scores{b}") for b in range(2)]
+        for b in range(2):
+            for h in range(2):
+                product(scores[b][:, h * HALF : (h + 1) * HALF], q_mx[b], k_mx[h])
 
         size_bank = bank("size_bank")
         for t in range(PACK):
             nc.tensor.transpose(size_bank[:, t * P : (t + 1) * P], size_cols[:, t : t + 1].to_broadcast([P, P]), ident[:])
         size_dealt = size_bank[:].rearrange("p (u r s) -> p u s r", u=2, r=2)
 
-        km_bf = [sbuf(f"km_bf{h}", [P, HALF, PACK], BF16) for h in range(2)]
-        k_codes = [sbuf(f"k_codes{h}", [P, HALF], U32) for h in range(2)]
-        k_scales = [sbuf(f"k_scales{h}", [P, HALF], U8) for h in range(2)]
-        q_bf = [sbuf(f"q_bf{b}", [P, P, PACK], BF16) for b in range(2)]
-        q_codes = [sbuf(f"q_codes{b}", [P, P], U32) for b in range(2)]
-        q_scales = [sbuf(f"q_scales{b}", [P, P], U8) for b in range(2)]
-        weave(nc.scalar.copy, km_bf[0][:], km[0][:])
-        weave(nc.vector.tensor_copy, q_bf[0][:], query_raw[:, :, 0:P])
-        weave(nc.vector.tensor_copy, km_bf[1][:], km[1][:])
-        weave(nc.scalar.copy, q_bf[1][:], query_raw[:, :, P:Q])
-        quantize(q_codes[0][:], q_scales[0][:], q_bf[0][:])
-        quantize(k_codes[0][:], k_scales[0][:], km_bf[0][:])
-        quantize(k_codes[1][:], k_scales[1][:], km_bf[1][:])
-        quantize(q_codes[1][:], q_scales[1][:], q_bf[1][:])
+        picked = [sbuf(f"picked{t}", [P, I], BF16)[:] for t in range(PACK - 1)]
+        overlap_at = (I - QUARTER) // 2
+        picked3_probs0 = sbuf("picked3_probs0", [P, overlap_at + I], F32)
+        picked.append(picked3_probs0[:, 0:HALF].bitcast(BF16))
 
-        scores = [bank(f"scores{b}") for b in range(2)]
-        for b in range(2):
-            for h in range(2):
-                nc.tensor.matmul_mx(out=scores[b][:, h * HALF : (h + 1) * HALF], lhsT=q_codes[b][:].bitcast(FP8X4), lhsT_scale=q_scales[b][:],
-                                    rhs=k_codes[h][:].bitcast(FP8X4), rhs_scale=k_scales[h][:], start=True, stop=True)
+        def pick(t, start, stop):
+            nc.vector.tensor_copy(picked[t][:, start:stop], listed(val_pool[t], start, stop))
 
-        picked = {t: pick(t) for t in (1,)}
+        pick(0, 0, I)
+        narrow = sbuf("narrow", [P, T], BF16)
+        nc.scalar.activation(narrow[:], val_pool[1][:], ACT.Copy)
+        nc.scalar.activation(picked[1], listed(narrow, 0, I), ACT.Copy)
+        pick(2, 0, HALF)
+        pick(2, HALF, I)
+
         neg_max = sbuf("neg_max", [P, 2], F32, "val_pool1")
         sums = [sbuf(f"sums{b}", [P, 1], F32) for b in range(2)]
-        inv = [sbuf(f"inv{b}", [P, 1], F32, (None, None)[b]) for b in range(2)]
-        probs = [sbuf(f"probs{b}", [P, 2, P, 2], F32) for b in range(2)]
+        inv = [sbuf(f"inv{b}", [P, 1], F32) for b in range(2)]
+        probs = [flat.rearrange("p (u s r) -> p u s r", u=2, r=2)
+                 for flat in (picked3_probs0[:, overlap_at : overlap_at + I], sbuf("probs1", [P, I], F32)[:])]
         for b in range(2):
             nc.vector.tensor_reduce(neg_max[:, b : b + 1], scores[b][:], AX.X, ALU.max, negate=True)
-            nc.scalar.activation(probs[b][:], scores[b][:].rearrange("p (s u r) -> p u s r", u=2, r=2), ACT.Exp,
+            nc.scalar.activation(probs[b], scores[b][:].rearrange("p (s u r) -> p u s r", u=2, r=2), ACT.Exp,
                                  bias=neg_max[:, b : b + 1], accum_out=sums[b][:])
-        for t in ():
-            picked[t] = pick(t)
 
-        w_bf = [[sbuf(f"w_bf{b}_{u}", [P, P, 2], BF16, {}.get((b, u))) for u in range(2)] for b in range(2)]
-        for b in range(2):
-            nc.vector.reciprocal(inv[b][:], sums[b][:])
+        w_bf = [[sbuf(f"w_bf{b}_{u}", [P, P, 2], BF16) for u in range(2)] for b in range(2)]
+
+        def weights(b):
             for u in range(2):
                 nc.vector.scalar_tensor_tensor(w_bf[b][u][:], probs[b][:, u], inv[b][:], size_dealt[:, u], ALU.mult, ALU.mult)
-        w_ops = [
-            turn([w_bf[b][u][:].rearrange("p s r -> p (s r)").bitcast(F32) for u in range(2)], bank(f"w_turned{b}", tag=f"scores{b}"), f"w{b}")
-            for b in range(2)
-        ]
-        for t in (0, 2, 3):
-            picked[t] = pick(t)
-        v_ops = [values(t, picked[t]) for t in range(PACK)]
+
+        pick(3, 0, HALF)
+        nc.vector.reciprocal(inv[0][:], sums[0][:])
+        pick(3, HALF, I - QUARTER)
+        nc.vector.reciprocal(inv[1][:], sums[1][:])
+        weights(0)
+        pick(3, I - QUARTER, I)
+        weights(1)
+
+        def turn(name, word_halves, bank_of, scales):
+            turned = bank(name + "_turned", bank_of)
+            for u in range(2):
+                nc.tensor.transpose(turned[:, u * P : (u + 1) * P], word_halves[u], ident[:])
+            words = sbuf(name + "_words", [P, P, 2], F32)
+            nc.scalar.copy(out=words[:], in_=turned[:, 0 : 2 * P].rearrange("p (u c) -> p c u", u=2))
+            codes = sbuf(name + "_codes", [P, P], U32)[:]
+            nc.vector.quantize_mx(out=codes.bitcast(FP8X4), scales=scales, in_=words[:].rearrange("p c u -> p (c u)").bitcast(BF16))
+            return codes, scales
+
+        early_scales = sbuf("early_scales", [P, (PACK - 1) * P], U8, "inv0")
+        v_scales = [early_scales[:, t * P : (t + 1) * P] for t in range(PACK - 1)] + [sbuf("v3_scales", [P, P], U8)[:]]
+
+        def turn_values(t, bank_of=None):
+            words = picked[t].bitcast(F32)
+            return turn(f"v{t}", [words[:, u : 2 * P : 2] for u in range(2)], bank_of, v_scales[t])
+
+        def turn_weights(b, bank_of=None):
+            halves = [w_bf[b][u][:].rearrange("p s r -> p (s r)").bitcast(F32) for u in range(2)]
+            return turn(f"w{b}", halves, bank_of, sbuf(f"w{b}_scales", [P, P], U8)[:])
+
+        v_mx, w_mx = {}, {}
+        v_mx[0] = turn_values(0, "scores0")
+        v_mx[2] = turn_values(2)
+        v_mx[1] = turn_values(1)
+        w_mx[0] = turn_weights(0, "scores1")
+        v_mx[3] = turn_values(3)
+        w_mx[1] = turn_weights(1)
 
         o_codes = sbuf("o_codes", [P, Q], U32)
         o_scales = sbuf("o_scales", [P, Q], U8)
         out_rows = out_0.rearrange("(p t) q -> p t q", t=PACK)
         out_words = out_1.rearrange("z p c r -> p (z c r)").bitcast(I32)
-        acc_tags = [["acc_x", "acc_y"], ["scores0", "size_bank"]]
-        for b in range(2):
-            cols = slice(b * P, (b + 1) * P)
-            result = sbuf(f"result{b}", [P, PACK, P], F32)
-            for pair in range(2):
-                acc = bank(f"acc{b}_{pair}", tag=acc_tags[b][pair])
-                for r in range(2):
-                    t = 2 * pair + r
-                    nc.tensor.matmul_mx(out=acc[:, r * P : (r + 1) * P], lhsT=v_ops[t][0][:].bitcast(FP8X4), lhsT_scale=v_ops[t][1][:],
-                                        rhs=w_ops[b][0][:].bitcast(FP8X4), rhs_scale=w_ops[b][1][:], start=True, stop=True)
-                rows = slice(2 * pair, 2 * pair + 2)
-                nc.scalar.copy(out=result[:, rows, :].rearrange("p t q -> p (t q)"), in_=acc[:, 0 : 2 * P])
-                nc.sync.dma_start(out_rows[:, rows, cols], result[:, rows, :])
-            result_bf = sbuf(f"result_bf{b}", [P, P, PACK], BF16)
-            weave(nc.vector.tensor_copy, result_bf[:], result[:])
-            quantize(o_codes[:, cols], o_scales[:, cols], result_bf[:])
+        result = sbuf("result", [P, PACK, Q], F32)
+        result_bf = sbuf("result_bf", [P, Q, PACK], BF16)
+
+        def result_planes(b, first, stop, bank_of, copy):
+            acc = bank(f"acc{b}_{first}", bank_of)
+            for t in range(first, stop):
+                product(acc[:, (t - first) * P : (t - first + 1) * P], v_mx[t], w_mx[b])
+            copy(out=result[:, first:stop, b * P : (b + 1) * P], in_=acc[:, 0 : (stop - first) * P].rearrange("p (t q) -> p t q", q=P))
+
+        def store_result(b):
+            nc.sync.dma_start(out_rows[:, :, b * P : (b + 1) * P], result[:, :, b * P : (b + 1) * P])
+
+        result_planes(0, 0, 3, None, nc.scalar.copy)
+        result_planes(0, 3, 4, "size_bank", nc.vector.tensor_copy)
+        store_result(0)
+        result_planes(1, 0, 2, "v1_turned", nc.vector.tensor_copy)
+        result_planes(1, 2, 3, "v2_turned", nc.scalar.copy)
+        result_planes(1, 3, 4, "scores0", nc.scalar.copy)
+        store_result(1)
+
+        def hand_on(start, widths):
+            pieces = [slice(start + sum(widths[:n]), start + sum(widths[: n + 1])) for n in range(len(widths))]
+            for cols in pieces:
+                weave(nc.vector.tensor_copy, result_bf[:, cols, :], result[:, :, cols])
+            for cols in pieces:
+                quantize(o_codes[:, cols], o_scales[:, cols], result_bf[:, cols, :])
+            cols = slice(start, start + sum(widths))
             nc.sync.dma_start(out_words[:, cols], o_codes[:, cols].bitcast(I32))
+
+        hand_on(0, [P])
+        hand_on(P, [P // 2, P // 2])
         for g in range(4):
             queue = nc.sync if g % 2 == 0 else nc.scalar
             queue.dma_start(out_2[0, 4 * g : 4 * g + 4, :].bitcast(I32), o_scales[32 * g : 32 * g + 4, :].bitcast(I32))

@@ -193,28 +193,23 @@ def tile_attend_gatedkeys_pl_kernel(tc, query, keys, kgate, size, vals, offs, ou
                 product(acc[:, (t - first) * P : (t - first + 1) * P], v_mx[t], w_mx[b])
             copy(out=result[:, first:stop, b * P : (b + 1) * P], in_=acc[:, 0 : (stop - first) * P].rearrange("p (t q) -> p t q", q=P))
 
-        def store_result(b):
-            nc.sync.dma_start(out_rows[:, :, b * P : (b + 1) * P], result[:, :, b * P : (b + 1) * P])
+        def store_planes(first, stop):
+            nc.sync.dma_start(out_rows[:, first:stop, :], result[:, first:stop, :])
 
         result_planes(0, 0, 3, None, nc.scalar.copy)
         result_planes(0, 3, 4, "size_bank", nc.vector.tensor_copy)
-        store_result(0)
         result_planes(1, 0, 2, "v1_turned", nc.vector.tensor_copy)
+        store_planes(0, 2)
         result_planes(1, 2, 3, "v2_turned", nc.scalar.copy)
         result_planes(1, 3, 4, "scores0", nc.scalar.copy)
-        store_result(1)
+        store_planes(2, 4)
 
-        def hand_on(start, widths):
-            pieces = [slice(start + sum(widths[:n]), start + sum(widths[: n + 1])) for n in range(len(widths))]
-            for cols in pieces:
-                weave(nc.vector.tensor_copy, result_bf[:, cols, :], result[:, :, cols])
-            for cols in pieces:
-                quantize(o_codes[:, cols], o_scales[:, cols], result_bf[:, cols, :])
-            cols = slice(start, start + sum(widths))
-            nc.sync.dma_start(out_words[:, cols], o_codes[:, cols].bitcast(I32))
-
-        hand_on(0, [P])
-        hand_on(P, [P // 2, P // 2])
+        blocks = [slice(b * P, (b + 1) * P) for b in range(2)]
+        for cols in blocks:
+            weave(nc.vector.tensor_copy, result_bf[:, cols, :], result[:, :, cols])
+        for cols in blocks:
+            quantize(o_codes[:, cols], o_scales[:, cols], result_bf[:, cols, :])
+        nc.sync.dma_start(out_words, o_codes[:].bitcast(I32))
         for g in range(4):
             queue = nc.sync if g % 2 == 0 else nc.scalar
             queue.dma_start(out_2[0, 4 * g : 4 * g + 4, :].bitcast(I32), o_scales[32 * g : 32 * g + 4, :].bitcast(I32))

@@ -74,38 +74,36 @@ def tile_attend_gatedkeys_pl_kernel(tc, query, keys, kgate, size, vals, offs, ou
         def listed(pool_tile, start, stop):
             return pool_tile[:].indirect(offsets[:, start // LIST_ROWS : stop // LIST_ROWS])
 
-        gates = [[sbuf(f"gate{t}_{h}", [P, HALF], F32) for h in range(2)] for t in range(PACK)]
-        km = [sbuf(f"km{h}", [P, PACK, HALF], F32) for h in range(2)]
+        gates = [sbuf(f"gate{t}", [P, I], F32) for t in range(PACK)]
+        km = sbuf("km", [P, PACK, I], F32)
+        halves = [slice(h * HALF, (h + 1) * HALF) for h in range(2)]
         for t in range(PACK):
-            for h in range(2):
-                nc.scalar.activation(gates[t][h][:], listed(gate_pool[t], h * HALF, (h + 1) * HALF), ACT.Sigmoid)
-            for h in range(2):
-                nc.vector.tensor_tensor(km[h][:, t, :], listed(key_pool[t], h * HALF, (h + 1) * HALF), gates[t][h][:], ALU.mult)
+            pieces = halves if t == PACK - 1 else [slice(0, I)]
+            for cols in pieces:
+                nc.scalar.activation(gates[t][:, cols], listed(gate_pool[t], cols.start, cols.stop), ACT.Sigmoid)
+            for cols in pieces:
+                nc.vector.tensor_tensor(km[:, t, cols], listed(key_pool[t], cols.start, cols.stop), gates[t][:, cols], ALU.mult)
         exp_warm = sbuf("exp_warm", [P, 1], F32)
-        nc.scalar.activation(exp_warm[:], gates[PACK - 1][0][:, 0:1], ACT.Exp)
+        nc.scalar.activation(exp_warm[:], gates[PACK - 1][:, 0:1], ACT.Exp)
 
         q_bf = [sbuf(f"q_bf{b}", [P, P, PACK], BF16) for b in range(2)]
         km_bf = [sbuf("km_bf0", [P, HALF, PACK], BF16)]
         for b in range(2):
             weave(nc.scalar.copy, q_bf[b][:], query_raw[:, :, b * P : (b + 1) * P])
-        for c in range(2):
-            weave(nc.vector.tensor_copy, km_bf[0][:, c * QUARTER : (c + 1) * QUARTER, :], km[0][:, :, c * QUARTER : (c + 1) * QUARTER])
+        weave(nc.vector.tensor_copy, km_bf[0][:], km[:, :, halves[0]])
         km_bf.append(sbuf("km_bf1", [P, HALF, PACK], BF16, "query_raw"))
-        weave(nc.scalar.copy, km_bf[1][:], km[1][:])
+        weave(nc.scalar.copy, km_bf[1][:], km[:, :, halves[1]])
 
         k_mx = [(sbuf(f"k_codes{h}", [P, HALF], U32)[:], sbuf(f"k_scales{h}", [P, HALF], U8)[:]) for h in range(2)]
         q_mx = [(sbuf(f"q_codes{b}", [P, P], U32)[:], sbuf(f"q_scales{b}", [P, P], U8)[:]) for b in range(2)]
-        quantize(*q_mx[0], q_bf[0][:])
-        for c in range(2):
-            cols = slice(c * QUARTER, (c + 1) * QUARTER)
-            quantize(k_mx[0][0][:, cols], k_mx[0][1][:, cols], km_bf[0][:, cols, :])
-        quantize(*q_mx[1], q_bf[1][:])
-        quantize(*k_mx[1], km_bf[1][:])
+        for n in range(2):
+            quantize(*q_mx[n], q_bf[n][:])
+            quantize(*k_mx[n], km_bf[n][:])
 
         scores = [bank(f"scores{b}") for b in range(2)]
         for b in range(2):
             for h in range(2):
-                product(scores[b][:, h * HALF : (h + 1) * HALF], q_mx[b], k_mx[h])
+                product(scores[b][:, halves[h]], q_mx[b], k_mx[h])
 
         size_bank = bank("size_bank")
         for t in range(PACK):
@@ -124,8 +122,7 @@ def tile_attend_gatedkeys_pl_kernel(tc, query, keys, kgate, size, vals, offs, ou
         narrow = sbuf("narrow", [P, T], BF16)
         nc.scalar.activation(narrow[:], val_pool[1][:], ACT.Copy)
         nc.scalar.activation(picked[1], listed(narrow, 0, I), ACT.Copy)
-        pick(2, 0, HALF)
-        pick(2, HALF, I)
+        pick(2, 0, I)
 
         neg_max = sbuf("neg_max", [P, 2], F32, "val_pool1")
         sums = [sbuf(f"sums{b}", [P, 1], F32) for b in range(2)]

@@ -18,7 +18,6 @@ D, T, I, Q, E = 512, 1024, 512, 256, 512
 P = 128
 PACK = 4
 HALF = I // 2
-QUARTER = I // 4
 LIST_ROWS = 16
 FLOPS = 2 * D * Q * I + 2 * I * E * Q
 
@@ -50,7 +49,10 @@ def tile_attend_gatedkeys_pl_kernel(tc, query, keys, kgate, size, vals, offs, ou
         gate_pool = [sbuf(f"gate_pool{t}", [P, T], F32) for t in range(PACK)]
         key_pool = [sbuf(f"key_pool{t}", [P, T], F32) for t in range(PACK)]
         val_pool = [sbuf(f"val_pool{t}", [P, T], F32) for t in range(PACK)]
-        query_raw = sbuf("query_raw", [P, PACK, Q], F32)
+        km_words, overlap = I * PACK // 2, 16
+        km_query = sbuf("km_query", [P, km_words - overlap + PACK * Q], F32)
+        km_bf = km_query[:, 0:km_words].bitcast(BF16).rearrange("p (c t) -> p c t", t=PACK)
+        query_raw = km_query[:, km_words - overlap :].rearrange("p (t q) -> p t q", t=PACK)
         size_cols = sbuf("size_cols", [P, PACK], F32)
 
         def load_plane(pool, source, t):
@@ -62,7 +64,7 @@ def tile_attend_gatedkeys_pl_kernel(tc, query, keys, kgate, size, vals, offs, ou
         for pool, source in ((gate_pool, kgate), (key_pool, keys)):
             for t in range(2, PACK):
                 load_plane(pool, source, t)
-        nc.sync.dma_start(query_raw[:], query.rearrange("(p t) q -> p t q", t=PACK))
+        nc.sync.dma_start(query_raw, query.rearrange("(p t) q -> p t q", t=PACK))
         for t in range(PACK - 1):
             load_plane(val_pool, vals, t)
         nc.sync.dma_start(size_cols[:], size.rearrange("o (p t) -> p (o t)", t=PACK))
@@ -78,42 +80,33 @@ def tile_attend_gatedkeys_pl_kernel(tc, query, keys, kgate, size, vals, offs, ou
         km = sbuf("km", [P, PACK, I], F32)
         halves = [slice(h * HALF, (h + 1) * HALF) for h in range(2)]
         for t in range(PACK):
-            pieces = halves if t == PACK - 1 else [slice(0, I)]
-            for cols in pieces:
-                nc.scalar.activation(gates[t][:, cols], listed(gate_pool[t], cols.start, cols.stop), ACT.Sigmoid)
-            for cols in pieces:
+            nc.scalar.activation(gates[t][:], listed(gate_pool[t], 0, I), ACT.Sigmoid)
+            for cols in halves if t == PACK - 1 else [slice(0, I)]:
                 nc.vector.tensor_tensor(km[:, t, cols], listed(key_pool[t], cols.start, cols.stop), gates[t][:, cols], ALU.mult)
         exp_warm = sbuf("exp_warm", [P, 1], F32)
-        nc.scalar.activation(exp_warm[:], gates[PACK - 1][:, 0:1], ACT.Exp)
+        nc.scalar.activation(exp_warm[:], gate_pool[PACK - 1][:, 0:1], ACT.Exp)
 
-        q_bf = [sbuf(f"q_bf{b}", [P, P, PACK], BF16) for b in range(2)]
-        km_bf = [sbuf("km_bf0", [P, HALF, PACK], BF16)]
-        for b in range(2):
-            weave(nc.scalar.copy, q_bf[b][:], query_raw[:, :, b * P : (b + 1) * P])
-        weave(nc.vector.tensor_copy, km_bf[0][:], km[:, :, halves[0]])
-        km_bf.append(sbuf("km_bf1", [P, HALF, PACK], BF16, "query_raw"))
-        weave(nc.scalar.copy, km_bf[1][:], km[:, :, halves[1]])
-
-        k_mx = [(sbuf(f"k_codes{h}", [P, HALF], U32)[:], sbuf(f"k_scales{h}", [P, HALF], U8)[:]) for h in range(2)]
-        q_mx = [(sbuf(f"q_codes{b}", [P, P], U32)[:], sbuf(f"q_scales{b}", [P, P], U8)[:]) for b in range(2)]
-        for n in range(2):
-            quantize(*q_mx[n], q_bf[n][:])
-            quantize(*k_mx[n], km_bf[n][:])
+        blocks = [slice(b * P, (b + 1) * P) for b in range(2)]
+        q_bf = sbuf("q_bf", [P, Q, PACK], BF16)
+        for cols in blocks:
+            weave(nc.scalar.copy, q_bf[:, cols, :], query_raw[:, :, cols])
+        for copy, cols in zip((nc.vector.tensor_copy, nc.scalar.copy), halves):
+            weave(copy, km_bf[:, cols, :], km[:, :, cols])
+        q_codes, q_scales = sbuf("q_codes", [P, Q], U32), sbuf("q_scales", [P, Q], U8)
+        k_codes, k_scales = sbuf("k_codes", [P, I], U32), sbuf("k_scales", [P, I], U8)
+        quantize(q_codes[:], q_scales[:], q_bf[:])
+        quantize(k_codes[:], k_scales[:], km_bf)
 
         scores = [bank(f"scores{b}") for b in range(2)]
         for b in range(2):
-            for h in range(2):
-                product(scores[b][:, halves[h]], q_mx[b], k_mx[h])
+            product(scores[b][:], (q_codes[:, blocks[b]], q_scales[:, blocks[b]]), (k_codes[:], k_scales[:]))
 
         size_bank = bank("size_bank")
         for t in range(PACK):
             nc.tensor.transpose(size_bank[:, t * P : (t + 1) * P], size_cols[:, t : t + 1].to_broadcast([P, P]), ident[:])
         size_dealt = size_bank[:].rearrange("p (u r s) -> p u s r", u=2, r=2)
 
-        picked = [sbuf(f"picked{t}", [P, I], BF16)[:] for t in range(PACK - 1)]
-        overlap_at = (I - QUARTER) // 2
-        picked3_probs0 = sbuf("picked3_probs0", [P, overlap_at + I], F32)
-        picked.append(picked3_probs0[:, 0:HALF].bitcast(BF16))
+        picked = [sbuf(f"picked{t}", [P, I], BF16)[:] for t in range(PACK)]
 
         def pick(t, start, stop):
             nc.vector.tensor_copy(picked[t][:, start:stop], listed(val_pool[t], start, stop))
@@ -127,26 +120,20 @@ def tile_attend_gatedkeys_pl_kernel(tc, query, keys, kgate, size, vals, offs, ou
         neg_max = sbuf("neg_max", [P, 2], F32, "val_pool1")
         sums = [sbuf(f"sums{b}", [P, 1], F32) for b in range(2)]
         inv = [sbuf(f"inv{b}", [P, 1], F32) for b in range(2)]
-        probs = [flat.rearrange("p (u s r) -> p u s r", u=2, r=2)
-                 for flat in (picked3_probs0[:, overlap_at : overlap_at + I], sbuf("probs1", [P, I], F32)[:])]
+        probs = [sbuf(f"probs{b}", [P, 2, P, 2], F32) for b in range(2)]
         for b in range(2):
             nc.vector.tensor_reduce(neg_max[:, b : b + 1], scores[b][:], AX.X, ALU.max, negate=True)
-            nc.scalar.activation(probs[b], scores[b][:].rearrange("p (s u r) -> p u s r", u=2, r=2), ACT.Exp,
+            nc.scalar.activation(probs[b][:], scores[b][:].rearrange("p (s u r) -> p u s r", u=2, r=2), ACT.Exp,
                                  bias=neg_max[:, b : b + 1], accum_out=sums[b][:])
-
-        w_bf = [[sbuf(f"w_bf{b}_{u}", [P, P, 2], BF16) for u in range(2)] for b in range(2)]
-
-        def weights(b):
-            for u in range(2):
-                nc.vector.scalar_tensor_tensor(w_bf[b][u][:], probs[b][:, u], inv[b][:], size_dealt[:, u], ALU.mult, ALU.mult)
 
         pick(3, 0, HALF)
         nc.vector.reciprocal(inv[0][:], sums[0][:])
-        pick(3, HALF, I - QUARTER)
+        pick(3, HALF, I)
         nc.vector.reciprocal(inv[1][:], sums[1][:])
-        weights(0)
-        pick(3, I - QUARTER, I)
-        weights(1)
+        w_bf = [[sbuf(f"w_bf{b}_{u}", [P, P, 2], BF16) for u in range(2)] for b in range(2)]
+        for b in range(2):
+            for u in range(2):
+                nc.vector.scalar_tensor_tensor(w_bf[b][u][:], probs[b][:, u], inv[b][:], size_dealt[:, u], ALU.mult, ALU.mult)
 
         def turn(name, word_halves, bank_of, scales):
             turned = bank(name + "_turned", bank_of)
@@ -173,8 +160,8 @@ def tile_attend_gatedkeys_pl_kernel(tc, query, keys, kgate, size, vals, offs, ou
         v_mx[0] = turn_values(0, "scores0")
         v_mx[2] = turn_values(2)
         v_mx[1] = turn_values(1)
-        w_mx[0] = turn_weights(0, "scores1")
         v_mx[3] = turn_values(3)
+        w_mx[0] = turn_weights(0, "scores1")
         w_mx[1] = turn_weights(1)
 
         o_codes = sbuf("o_codes", [P, Q], U32)
@@ -201,7 +188,6 @@ def tile_attend_gatedkeys_pl_kernel(tc, query, keys, kgate, size, vals, offs, ou
         result_planes(1, 3, 4, "scores0", nc.scalar.copy)
         store_planes(2, 4)
 
-        blocks = [slice(b * P, (b + 1) * P) for b in range(2)]
         for cols in blocks:
             weave(nc.vector.tensor_copy, result_bf[:, cols, :], result[:, :, cols])
         for cols in blocks:

@@ -18,6 +18,7 @@ D, T, I, Q, E = 512, 1024, 512, 256, 512
 P = 128
 PACK = 4
 HALF = I // 2
+RUN = 16
 LIST_ROWS = 16
 FLOPS = 2 * D * Q * I + 2 * I * E * Q
 
@@ -103,34 +104,37 @@ def tile_attend_gatedkeys_pl_kernel(tc, query, keys, kgate, size, vals, offs, ou
 
         size_bank = bank("size_bank")
         for t in range(PACK):
-            nc.tensor.transpose(size_bank[:, t * P : (t + 1) * P], size_cols[:, t : t + 1].to_broadcast([P, P]), ident[:])
-        size_dealt = size_bank[:].rearrange("p (u r s) -> p u s r", u=2, r=2)
+            nc.tensor.transpose(size_bank[:, t : I : PACK], size_cols[:, t : t + 1].to_broadcast([P, P]), ident[:])
+        size_dealt = size_bank[:].rearrange("p (g u x) -> p u g x", u=2, x=RUN)
 
         picked = [sbuf(f"picked{t}", [P, I], BF16)[:] for t in range(PACK)]
 
+        def dealt(tile):
+            return tile.rearrange("p (u g x) -> p g u x", u=2, x=RUN)
+
         def pick(t, start, stop):
-            nc.vector.tensor_copy(picked[t][:, start:stop], listed(val_pool[t], start, stop))
+            nc.vector.tensor_copy(dealt(picked[t])[:, start // (2 * RUN) : stop // (2 * RUN)], listed(val_pool[t], start, stop))
 
         pick(0, 0, I)
         narrow = sbuf("narrow", [P, T], BF16)
         nc.scalar.activation(narrow[:], val_pool[1][:], ACT.Copy)
-        nc.scalar.activation(picked[1], listed(narrow, 0, I), ACT.Copy)
+        nc.scalar.activation(dealt(picked[1]), listed(narrow, 0, I), ACT.Copy)
         pick(2, 0, I)
 
         neg_max = sbuf("neg_max", [P, 2], F32, "val_pool1")
         sums = [sbuf(f"sums{b}", [P, 1], F32) for b in range(2)]
         inv = [sbuf(f"inv{b}", [P, 1], F32) for b in range(2)]
-        probs = [sbuf(f"probs{b}", [P, 2, P, 2], F32) for b in range(2)]
+        probs = [sbuf(f"probs{b}", [P, 2, I // (2 * RUN), RUN], F32) for b in range(2)]
         for b in range(2):
             nc.vector.tensor_reduce(neg_max[:, b : b + 1], scores[b][:], AX.X, ALU.max, negate=True)
-            nc.scalar.activation(probs[b][:], scores[b][:].rearrange("p (s u r) -> p u s r", u=2, r=2), ACT.Exp,
+            nc.scalar.activation(probs[b][:], scores[b][:].rearrange("p (g u x) -> p u g x", u=2, x=RUN), ACT.Exp,
                                  bias=neg_max[:, b : b + 1], accum_out=sums[b][:])
 
         pick(3, 0, HALF)
         nc.vector.reciprocal(inv[0][:], sums[0][:])
         pick(3, HALF, I)
         nc.vector.reciprocal(inv[1][:], sums[1][:])
-        w_bf = [[sbuf(f"w_bf{b}_{u}", [P, P, 2], BF16) for u in range(2)] for b in range(2)]
+        w_bf = [[sbuf(f"w_bf{b}_{u}", [P, I // (2 * RUN), RUN], BF16) for u in range(2)] for b in range(2)]
         for b in range(2):
             for u in range(2):
                 nc.vector.scalar_tensor_tensor(w_bf[b][u][:], probs[b][:, u], inv[b][:], size_dealt[:, u], ALU.mult, ALU.mult)
@@ -150,7 +154,7 @@ def tile_attend_gatedkeys_pl_kernel(tc, query, keys, kgate, size, vals, offs, ou
 
         def turn_values(t, bank_of=None):
             words = picked[t].bitcast(F32)
-            return turn(f"v{t}", [words[:, u : 2 * P : 2] for u in range(2)], bank_of, v_scales[t])
+            return turn(f"v{t}", [words[:, u * P : (u + 1) * P] for u in range(2)], bank_of, v_scales[t])
 
         def turn_weights(b, bank_of=None):
             halves = [w_bf[b][u][:].rearrange("p s r -> p (s r)").bitcast(F32) for u in range(2)]

@@ -46,7 +46,6 @@ def tile_attend_gatedkeys_pl_kernel(tc, query, keys, kgate, size, vals, offs, ou
                                 rhs=moving[0].bitcast(FP8X4), rhs_scale=moving[1], start=True, stop=True)
 
         offsets = sbuf("offsets", [P, I // LIST_ROWS], U16)
-        nc.sync.dma_start(offsets[:], offs)
         gate_pool = [sbuf(f"gate_pool{t}", [P, T], F32) for t in range(PACK)]
         key_pool = [sbuf(f"key_pool{t}", [P, T], F32) for t in range(PACK)]
         val_pool = [sbuf(f"val_pool{t}", [P, T], F32) for t in range(PACK)]
@@ -61,6 +60,8 @@ def tile_attend_gatedkeys_pl_kernel(tc, query, keys, kgate, size, vals, offs, ou
 
         for t in range(2):
             load_plane(gate_pool, kgate, t)
+            if t == 0:
+                nc.sync.dma_start(offsets[:], offs)
             load_plane(key_pool, keys, t)
         for pool, source in ((gate_pool, kgate), (key_pool, keys)):
             for t in range(2, PACK):
@@ -104,8 +105,8 @@ def tile_attend_gatedkeys_pl_kernel(tc, query, keys, kgate, size, vals, offs, ou
 
         size_bank = bank("size_bank")
         for t in range(PACK):
-            nc.tensor.transpose(size_bank[:, t : I : PACK], size_cols[:, t : t + 1].to_broadcast([P, P]), ident[:])
-        size_dealt = size_bank[:].rearrange("p (g u x) -> p u g x", u=2, x=RUN)
+            nc.tensor.transpose(size_bank[:].rearrange("p (u g a t) -> p t g u a", u=2, a=RUN // PACK, t=PACK)[:, t], size_cols[:, t : t + 1].to_broadcast([P, P]), ident[:])
+        size_dealt = size_bank[:].rearrange("p (u c) -> p u c", u=2)
 
         picked = [sbuf(f"picked{t}", [P, I], BF16)[:] for t in range(PACK)]
 
@@ -134,10 +135,11 @@ def tile_attend_gatedkeys_pl_kernel(tc, query, keys, kgate, size, vals, offs, ou
         nc.vector.reciprocal(inv[0][:], sums[0][:])
         pick(3, HALF, I)
         nc.vector.reciprocal(inv[1][:], sums[1][:])
-        w_bf = [[sbuf(f"w_bf{b}_{u}", [P, I // (2 * RUN), RUN], BF16) for u in range(2)] for b in range(2)]
-        for b in range(2):
-            for u in range(2):
-                nc.vector.scalar_tensor_tensor(w_bf[b][u][:], probs[b][:, u], inv[b][:], size_dealt[:, u], ALU.mult, ALU.mult)
+        w_bf = [sbuf(f"w_bf{b}", [P, 2, HALF], BF16) for b in range(2)]
+        flat = [probs[b][:].rearrange("p u g x -> p u (g x)") for b in range(2)]
+        nc.vector.scalar_tensor_tensor(w_bf[0][:], flat[0], inv[0][:], size_dealt, ALU.mult, ALU.mult)
+        for u in range(2):
+            nc.vector.scalar_tensor_tensor(w_bf[1][:, u], flat[1][:, u], inv[1][:], size_dealt[:, u], ALU.mult, ALU.mult)
 
         def turn(name, word_halves, bank_of, scales):
             turned = bank(name + "_turned", bank_of)
@@ -157,7 +159,7 @@ def tile_attend_gatedkeys_pl_kernel(tc, query, keys, kgate, size, vals, offs, ou
             return turn(f"v{t}", [words[:, u * P : (u + 1) * P] for u in range(2)], bank_of, v_scales[t])
 
         def turn_weights(b, bank_of=None):
-            halves = [w_bf[b][u][:].rearrange("p s r -> p (s r)").bitcast(F32) for u in range(2)]
+            halves = [w_bf[b][:, u].bitcast(F32) for u in range(2)]
             return turn(f"w{b}", halves, bank_of, sbuf(f"w{b}_scales", [P, P], U8)[:])
 
         v_mx, w_mx = {}, {}

@@ -18,7 +18,6 @@ D, T, I, Q, E = 512, 1024, 512, 256, 512
 P = 128
 PACK = 4
 HALF = I // 2
-RUN = 16
 LIST_ROWS = 16
 FLOPS = 2 * D * Q * I + 2 * I * E * Q
 
@@ -49,10 +48,7 @@ def tile_attend_gatedkeys_pl_kernel(tc, query, keys, kgate, size, vals, offs, ou
         gate_pool = [sbuf(f"gate_pool{t}", [P, T], F32) for t in range(PACK)]
         key_pool = [sbuf(f"key_pool{t}", [P, T], F32) for t in range(PACK)]
         val_pool = [sbuf(f"val_pool{t}", [P, T], F32) for t in range(PACK)]
-        km_words, overlap = I * PACK // 2, 16
-        km_query = sbuf("km_query", [P, km_words - overlap + PACK * Q], F32)
-        km_bf = km_query[:, 0:km_words].bitcast(BF16).rearrange("p (c t) -> p c t", t=PACK)
-        query_raw = km_query[:, km_words - overlap :].rearrange("p (t q) -> p t q", t=PACK)
+        query_raw = sbuf("query_raw", [P, PACK, Q], F32)
         size_cols = sbuf("size_cols", [P, PACK], F32)
 
         def load_plane(pool, source, t):
@@ -66,7 +62,7 @@ def tile_attend_gatedkeys_pl_kernel(tc, query, keys, kgate, size, vals, offs, ou
         for pool, source in ((gate_pool, kgate), (key_pool, keys)):
             for t in range(2, PACK):
                 load_plane(pool, source, t)
-        nc.sync.dma_start(query_raw, query.rearrange("(p t) q -> p t q", t=PACK))
+        nc.sync.dma_start(query_raw[:], query.rearrange("(p t) q -> p t q", t=PACK))
         for t in range(PACK - 1):
             load_plane(val_pool, vals, t)
         nc.sync.dma_start(size_cols[:], size.rearrange("o (p t) -> p (o t)", t=PACK))
@@ -89,86 +85,78 @@ def tile_attend_gatedkeys_pl_kernel(tc, query, keys, kgate, size, vals, offs, ou
         nc.scalar.activation(exp_warm[:], gate_pool[PACK - 1][:, 0:1], ACT.Exp)
 
         blocks = [slice(b * P, (b + 1) * P) for b in range(2)]
+        km_bf = sbuf("km_bf", [P, I, PACK], BF16)
         q_bf = sbuf("q_bf", [P, Q, PACK], BF16)
-        for cols in blocks:
-            weave(nc.scalar.copy, q_bf[:, cols, :], query_raw[:, :, cols])
-        for copy, cols in zip((nc.vector.tensor_copy, nc.scalar.copy), halves):
-            weave(copy, km_bf[:, cols, :], km[:, :, cols])
         q_codes, q_scales = sbuf("q_codes", [P, Q], U32), sbuf("q_scales", [P, Q], U8)
         k_codes, k_scales = sbuf("k_codes", [P, I], U32), sbuf("k_scales", [P, I], U8)
-        quantize(q_codes[:], q_scales[:], q_bf[:])
-        quantize(k_codes[:], k_scales[:], km_bf)
+        weave(nc.scalar.copy, km_bf[:, halves[0], :], km[:, :, halves[0]])
+        weave(nc.vector.tensor_copy, q_bf[:, blocks[0], :], query_raw[:, :, blocks[0]])
+        weave(nc.vector.tensor_copy, km_bf[:, halves[1], :], km[:, :, halves[1]])
+        weave(nc.scalar.copy, q_bf[:, blocks[1], :], query_raw[:, :, blocks[1]])
+        quantize(q_codes[:, blocks[0]], q_scales[:, blocks[0]], q_bf[:, blocks[0], :])
+        quantize(k_codes[:], k_scales[:], km_bf[:])
+        quantize(q_codes[:, blocks[1]], q_scales[:, blocks[1]], q_bf[:, blocks[1], :])
 
         scores = [bank(f"scores{b}") for b in range(2)]
         for b in range(2):
             product(scores[b][:], (q_codes[:, blocks[b]], q_scales[:, blocks[b]]), (k_codes[:], k_scales[:]))
 
+        picked = [sbuf(f"picked{t}", [P, I], BF16) for t in range(PACK)]
+        nc.scalar.activation(picked[0][:], listed(val_pool[0], 0, I), ACT.Copy)
+        for cols in halves:
+            nc.scalar.activation(picked[1][:, cols], listed(val_pool[1], cols.start, cols.stop), ACT.Copy)
+
         size_bank = bank("size_bank")
         for t in range(PACK):
-            nc.tensor.transpose(size_bank[:].rearrange("p (u g a t) -> p t g u a", u=2, a=RUN // PACK, t=PACK)[:, t], size_cols[:, t : t + 1].to_broadcast([P, P]), ident[:])
-        size_dealt = size_bank[:].rearrange("p (u c) -> p u c", u=2)
+            nc.tensor.transpose(size_bank[:].rearrange("p (u s r) -> p u r s", u=2, r=2)[:, t // 2, t % 2], size_cols[:, t : t + 1].to_broadcast([P, P]), ident[:])
 
-        picked = [sbuf(f"picked{t}", [P, I], BF16)[:] for t in range(PACK)]
-
-        def dealt(tile):
-            return tile.rearrange("p (u g x) -> p g u x", u=2, x=RUN)
-
-        def pick(t, start, stop):
-            nc.vector.tensor_copy(dealt(picked[t])[:, start // (2 * RUN) : stop // (2 * RUN)], listed(val_pool[t], start, stop))
-
-        pick(0, 0, I)
-        narrow = sbuf("narrow", [P, T], BF16)
-        nc.scalar.activation(narrow[:], val_pool[1][:], ACT.Copy)
-        nc.scalar.activation(dealt(picked[1]), listed(narrow, 0, I), ACT.Copy)
-        pick(2, 0, I)
-
-        neg_max = sbuf("neg_max", [P, 2], F32, "val_pool1")
-        sums = [sbuf(f"sums{b}", [P, 1], F32) for b in range(2)]
+        neg_max = sbuf("neg_max", [P, 2], F32)
+        both_sums = sbuf("sums", [P, 2], F32, "val_pool1")
+        sums = [both_sums[:, b : b + 1] for b in range(2)]
         inv = [sbuf(f"inv{b}", [P, 1], F32) for b in range(2)]
-        probs = [sbuf(f"probs{b}", [P, 2, I // (2 * RUN), RUN], F32) for b in range(2)]
+        probs = [sbuf(f"probs{b}", [P, 2, P, 2], F32) for b in range(2)]
+        def turn(name, word_halves, words, copy, bank_of=None):
+            turned = bank(name + "_turned", bank_of)
+            for j, word_half in enumerate(word_halves):
+                nc.tensor.transpose(turned[:, j * P : (j + 1) * P], word_half, ident[:])
+            copy(out=words.rearrange("p (n c u) -> p n c u", u=2, c=P), in_=turned[:, 0 : len(word_halves) * P].rearrange("p (n u c) -> p n c u", u=2, c=P))
+
+        def value_halves(t):
+            words = picked[t][:].bitcast(F32).rearrange("p (s u) -> p u s", u=2)
+            return [words[:, u] for u in range(2)]
+
+        def quantize_words(name, words, scales_of=None):
+            n = words.shape[1] // (2 * P)
+            codes, scales = sbuf(name + "_codes", [P, n * P], U32)[:], sbuf(name + "_scales", [P, n * P], U8, scales_of)[:]
+            nc.vector.quantize_mx(out=codes.bitcast(FP8X4), scales=scales, in_=words.bitcast(BF16))
+            return [(codes[:, j * P : (j + 1) * P], scales[:, j * P : (j + 1) * P]) for j in range(n)]
+
         for b in range(2):
             nc.vector.tensor_reduce(neg_max[:, b : b + 1], scores[b][:], AX.X, ALU.max, negate=True)
-            nc.scalar.activation(probs[b][:], scores[b][:].rearrange("p (g u x) -> p u g x", u=2, x=RUN), ACT.Exp,
-                                 bias=neg_max[:, b : b + 1], accum_out=sums[b][:])
-
-        pick(3, 0, HALF)
-        nc.vector.reciprocal(inv[0][:], sums[0][:])
-        pick(3, HALF, I)
-        nc.vector.reciprocal(inv[1][:], sums[1][:])
+            nc.scalar.activation(probs[b][:], scores[b][:].rearrange("p (s u r) -> p u s r", u=2, r=2), ACT.Exp,
+                                 bias=neg_max[:, b : b + 1], accum_out=sums[b])
+        nc.vector.tensor_copy(picked[2][:], listed(val_pool[2], 0, I))
+        for b in range(2):
+            nc.vector.reciprocal(inv[b][:], sums[b])
+        v01_words = sbuf("v01_words", [P, 4 * P], F32)[:]
+        turn("v01", value_halves(0) + value_halves(1), v01_words, nc.scalar.copy)
+        nc.scalar.activation(picked[3][:], listed(val_pool[3], 0, I), ACT.Copy)
         w_bf = [sbuf(f"w_bf{b}", [P, 2, HALF], BF16) for b in range(2)]
-        flat = [probs[b][:].rearrange("p u g x -> p u (g x)") for b in range(2)]
+        flat = [probs[b][:].rearrange("p u s r -> p u (s r)") for b in range(2)]
+        size_dealt = size_bank[:].rearrange("p (u c) -> p u c", u=2)
         nc.vector.scalar_tensor_tensor(w_bf[0][:], flat[0], inv[0][:], size_dealt, ALU.mult, ALU.mult)
         for u in range(2):
             nc.vector.scalar_tensor_tensor(w_bf[1][:, u], flat[1][:, u], inv[1][:], size_dealt[:, u], ALU.mult, ALU.mult)
 
-        def turn(name, word_halves, bank_of, scales):
-            turned = bank(name + "_turned", bank_of)
-            for u in range(2):
-                nc.tensor.transpose(turned[:, u * P : (u + 1) * P], word_halves[u], ident[:])
-            words = sbuf(name + "_words", [P, P, 2], F32)
-            nc.scalar.copy(out=words[:], in_=turned[:, 0 : 2 * P].rearrange("p (u c) -> p c u", u=2))
-            codes = sbuf(name + "_codes", [P, P], U32)[:]
-            nc.vector.quantize_mx(out=codes.bitcast(FP8X4), scales=scales, in_=words[:].rearrange("p c u -> p (c u)").bitcast(BF16))
-            return codes, scales
-
-        early_scales = sbuf("early_scales", [P, (PACK - 1) * P], U8, "inv0")
-        v_scales = [early_scales[:, t * P : (t + 1) * P] for t in range(PACK - 1)] + [sbuf("v3_scales", [P, P], U8)[:]]
-
-        def turn_values(t, bank_of=None):
-            words = picked[t].bitcast(F32)
-            return turn(f"v{t}", [words[:, u * P : (u + 1) * P] for u in range(2)], bank_of, v_scales[t])
-
-        def turn_weights(b, bank_of=None):
-            halves = [w_bf[b][:, u].bitcast(F32) for u in range(2)]
-            return turn(f"w{b}", halves, bank_of, sbuf(f"w{b}_scales", [P, P], U8)[:])
-
-        v_mx, w_mx = {}, {}
-        v_mx[0] = turn_values(0, "scores0")
-        v_mx[2] = turn_values(2)
-        v_mx[1] = turn_values(1)
-        v_mx[3] = turn_values(3)
-        w_mx[0] = turn_weights(0, "scores1")
-        w_mx[1] = turn_weights(1)
+        w_words = [sbuf(f"w{b}_words", [P, 2 * P], F32)[:] for b in range(2)]
+        v2_words, v3_words = sbuf("v2_words", [P, 2 * P], F32, "val_pool3")[:], sbuf("v3_words", [P, 2 * P], F32)[:]
+        turn("w0", [w_bf[0][:, u].bitcast(F32) for u in range(2)], w_words[0], nc.vector.tensor_copy, "scores0")
+        turn("v2", value_halves(2), v2_words, nc.scalar.copy, "v01_turned")
+        turn("w1", [w_bf[1][:, u].bitcast(F32) for u in range(2)], w_words[1], nc.scalar.copy, "scores1")
+        turn("v3", value_halves(3), v3_words, nc.scalar.copy)
+        v_mx = quantize_words("v01", v01_words, "probs0") + quantize_words("v2", v2_words)
+        w_mx = quantize_words("w0", w_words[0]) + quantize_words("w1", w_words[1])
+        v_mx = v_mx + quantize_words("v3", v3_words)
 
         o_codes = sbuf("o_codes", [P, Q], U32)
         o_scales = sbuf("o_scales", [P, Q], U8)
@@ -187,16 +175,15 @@ def tile_attend_gatedkeys_pl_kernel(tc, query, keys, kgate, size, vals, offs, ou
             nc.sync.dma_start(out_rows[:, first:stop, :], result[:, first:stop, :])
 
         result_planes(0, 0, 3, None, nc.scalar.copy)
-        result_planes(0, 3, 4, "size_bank", nc.vector.tensor_copy)
-        result_planes(1, 0, 2, "v1_turned", nc.vector.tensor_copy)
+        result_planes(1, 0, 3, None, nc.vector.tensor_copy)
         store_planes(0, 2)
-        result_planes(1, 2, 3, "v2_turned", nc.scalar.copy)
-        result_planes(1, 3, 4, "scores0", nc.scalar.copy)
+        result_planes(0, 3, 4, "size_bank", nc.scalar.copy)
+        result_planes(1, 3, 4, None, nc.vector.tensor_copy)
         store_planes(2, 4)
 
-        for cols in blocks:
-            weave(nc.vector.tensor_copy, result_bf[:, cols, :], result[:, :, cols])
-        for cols in blocks:
+        for copy, cols in zip((nc.scalar.copy, nc.vector.tensor_copy), blocks):
+            weave(copy, result_bf[:, cols, :], result[:, :, cols])
+        for cols in reversed(blocks):
             quantize(o_codes[:, cols], o_scales[:, cols], result_bf[:, cols, :])
         nc.sync.dma_start(out_words, o_codes[:].bitcast(I32))
         for g in range(4):

@@ -45,8 +45,9 @@ def tile_attend_gatedkeys_pl_kernel(tc, query, keys, kgate, size, vals, offs, ou
                                 rhs=moving[0].bitcast(FP8X4), rhs_scale=moving[1], start=True, stop=True)
 
         offsets = sbuf("offsets", [P, I // LIST_ROWS], U16)
-        gate_pool = [sbuf(f"gate_pool{t}", [P, T], F32) for t in range(PACK)]
-        key_pool = [sbuf(f"key_pool{t}", [P, T], F32) for t in range(PACK)]
+        gate_pair, key_pair = sbuf("gate_pair", [P, 2 * T], F32), sbuf("key_pair", [P, 2 * T], F32)
+        gate_pool = {t: sbuf(f"gate_pool{t}", [P, T], F32) for t in range(2, PACK)}
+        key_pool = {t: sbuf(f"key_pool{t}", [P, T], F32) for t in range(2, PACK)}
         val_pool = [sbuf(f"val_pool{t}", [P, T], F32) for t in range(PACK)]
         query_raw = sbuf("query_raw", [P, PACK, Q], F32)
         size_cols = sbuf("size_cols", [P, PACK], F32)
@@ -54,11 +55,9 @@ def tile_attend_gatedkeys_pl_kernel(tc, query, keys, kgate, size, vals, offs, ou
         def load_plane(pool, source, t):
             nc.sync.dma_start(pool[t][:], source.rearrange("(p t) n -> p t n", t=PACK)[:, t, :])
 
-        for t in range(2):
-            load_plane(gate_pool, kgate, t)
-            if t == 0:
-                nc.sync.dma_start(offsets[:], offs)
-            load_plane(key_pool, keys, t)
+        nc.sync.dma_start(gate_pair[:], kgate.rearrange("(p t) n -> p (t n)", t=PACK)[:, 0 : 2 * T])
+        nc.sync.dma_start(offsets[:], offs)
+        nc.sync.dma_start(key_pair[:], keys.rearrange("(p t) n -> p (t n)", t=PACK)[:, 0 : 2 * T])
         for pool, source in ((gate_pool, kgate), (key_pool, keys)):
             for t in range(2, PACK):
                 load_plane(pool, source, t)
@@ -77,7 +76,14 @@ def tile_attend_gatedkeys_pl_kernel(tc, query, keys, kgate, size, vals, offs, ou
         gates = [sbuf(f"gate{t}", [P, I], F32) for t in range(PACK)]
         km = sbuf("km", [P, PACK, I], F32)
         halves = [slice(h * HALF, (h + 1) * HALF) for h in range(2)]
-        for t in range(PACK):
+        gate1, key1 = sbuf("raw_gate1", [P, I], F32), sbuf("raw_key1", [P, I], F32)
+        nc.vector.tensor_copy(gate1[:], gate_pair[:, T : 2 * T].indirect(offsets[:]))
+        nc.scalar.activation(gates[0][:], listed(gate_pair, 0, I), ACT.Sigmoid)
+        nc.scalar.activation(gates[1][:], gate1[:], ACT.Sigmoid)
+        nc.vector.tensor_copy(key1[:], key_pair[:, T : 2 * T].indirect(offsets[:]))
+        nc.vector.tensor_tensor(km[:, 0], listed(key_pair, 0, I), gates[0][:], ALU.mult)
+        nc.vector.tensor_tensor(km[:, 1], key1[:], gates[1][:], ALU.mult)
+        for t in range(2, PACK):
             nc.scalar.activation(gates[t][:], listed(gate_pool[t], 0, I), ACT.Sigmoid)
             for cols in halves if t == PACK - 1 else [slice(0, I)]:
                 nc.vector.tensor_tensor(km[:, t, cols], listed(key_pool[t], cols.start, cols.stop), gates[t][:, cols], ALU.mult)

@@ -18,6 +18,8 @@ D, T, I, Q, E = 512, 1024, 512, 256, 512
 P = 128
 PACK = 4
 HALF = I // 2
+SHARE2 = 7 * I // 8
+SHARE = 3 * I // 4
 LIST_ROWS = 16
 FLOPS = 2 * D * Q * I + 2 * I * E * Q
 
@@ -76,6 +78,8 @@ def tile_attend_gatedkeys_pl_kernel(tc, query, keys, kgate, size, vals, offs, ou
         gates = [sbuf(f"gate{t}", [P, I], F32) for t in range(PACK)]
         km = sbuf("km", [P, PACK, I], F32)
         halves = [slice(h * HALF, (h + 1) * HALF) for h in range(2)]
+        quarter = [slice(j * I // 4, (j + 1) * I // 4) for j in range(4)]
+        last_pieces = [quarter[0], slice(quarter[1].start, quarter[2].stop), quarter[3]]
         gate1, key1 = sbuf("raw_gate1", [P, I], F32), sbuf("raw_key1", [P, I], F32)
         nc.vector.tensor_copy(gate1[:], gate_pair[:, T : 2 * T].indirect(offsets[:]))
         nc.scalar.activation(gates[0][:], listed(gate_pair, 0, I), ACT.Sigmoid)
@@ -85,7 +89,7 @@ def tile_attend_gatedkeys_pl_kernel(tc, query, keys, kgate, size, vals, offs, ou
         nc.vector.tensor_tensor(km[:, 1], key1[:], gates[1][:], ALU.mult)
         for t in range(2, PACK):
             nc.scalar.activation(gates[t][:], listed(gate_pool[t], 0, I), ACT.Sigmoid)
-            for cols in halves if t == PACK - 1 else [slice(0, I)]:
+            for cols in last_pieces if t == PACK - 1 else [slice(0, I)]:
                 nc.vector.tensor_tensor(km[:, t, cols], listed(key_pool[t], cols.start, cols.stop), gates[t][:, cols], ALU.mult)
         exp_warm = sbuf("exp_warm", [P, 1], F32)
         nc.scalar.activation(exp_warm[:], gate_pool[PACK - 1][:, 0:1], ACT.Exp)
@@ -95,37 +99,35 @@ def tile_attend_gatedkeys_pl_kernel(tc, query, keys, kgate, size, vals, offs, ou
         q_bf = sbuf("q_bf", [P, Q, PACK], BF16)
         q_codes, q_scales = sbuf("q_codes", [P, Q], U32), sbuf("q_scales", [P, Q], U8)
         k_codes, k_scales = sbuf("k_codes", [P, I], U32), sbuf("k_scales", [P, I], U8)
-        weave(nc.scalar.copy, km_bf[:, halves[0], :], km[:, :, halves[0]])
+        for cols in quarter[0:2]:
+            weave(nc.scalar.copy, km_bf[:, cols, :], km[:, :, cols])
+        for cols in quarter[2:4]:
+            weave(nc.vector.tensor_copy, km_bf[:, cols, :], km[:, :, cols])
         weave(nc.vector.tensor_copy, q_bf[:, blocks[0], :], query_raw[:, :, blocks[0]])
-        weave(nc.vector.tensor_copy, km_bf[:, halves[1], :], km[:, :, halves[1]])
         weave(nc.scalar.copy, q_bf[:, blocks[1], :], query_raw[:, :, blocks[1]])
-        quantize(q_codes[:, blocks[0]], q_scales[:, blocks[0]], q_bf[:, blocks[0], :])
-        quantize(k_codes[:], k_scales[:], km_bf[:])
-        quantize(q_codes[:, blocks[1]], q_scales[:, blocks[1]], q_bf[:, blocks[1], :])
+        for b in range(2):
+            quantize(k_codes[:, halves[b]], k_scales[:, halves[b]], km_bf[:, halves[b], :])
+            quantize(q_codes[:, blocks[b]], q_scales[:, blocks[b]], q_bf[:, blocks[b], :])
 
         scores = [bank(f"scores{b}") for b in range(2)]
         for b in range(2):
-            product(scores[b][:], (q_codes[:, blocks[b]], q_scales[:, blocks[b]]), (k_codes[:], k_scales[:]))
+            for cols in halves:
+                product(scores[b][:, cols], (q_codes[:, blocks[b]], q_scales[:, blocks[b]]), (k_codes[:, cols], k_scales[:, cols]))
 
         picked = [sbuf(f"picked{t}", [P, I], BF16) for t in range(PACK)]
-        nc.scalar.activation(picked[0][:], listed(val_pool[0], 0, I), ACT.Copy)
+        nc.scalar.activation(picked[0][:, 0:SHARE], listed(val_pool[0], 0, SHARE), ACT.Copy)
+        nc.vector.tensor_copy(picked[0][:, SHARE:I], listed(val_pool[0], SHARE, I))
         for cols in halves:
             nc.scalar.activation(picked[1][:, cols], listed(val_pool[1], cols.start, cols.stop), ACT.Copy)
 
-        size_bank = bank("size_bank")
-        for t in range(PACK):
-            nc.tensor.transpose(size_bank[:].rearrange("p (u s r) -> p u r s", u=2, r=2)[:, t // 2, t % 2], size_cols[:, t : t + 1].to_broadcast([P, P]), ident[:])
-
-        neg_max = sbuf("neg_max", [P, 2], F32)
-        both_sums = sbuf("sums", [P, 2], F32, "val_pool1")
-        sums = [both_sums[:, b : b + 1] for b in range(2)]
-        inv = [sbuf(f"inv{b}", [P, 1], F32) for b in range(2)]
-        probs = [sbuf(f"probs{b}", [P, 2, P, 2], F32) for b in range(2)]
-        def turn(name, word_halves, words, copy, bank_of=None):
+        def turn(name, word_halves, bank_of=None):
             turned = bank(name + "_turned", bank_of)
-            for j, word_half in enumerate(word_halves):
-                nc.tensor.transpose(turned[:, j * P : (j + 1) * P], word_half, ident[:])
-            copy(out=words.rearrange("p (n c u) -> p n c u", u=2, c=P), in_=turned[:, 0 : len(word_halves) * P].rearrange("p (n u c) -> p n c u", u=2, c=P))
+            for u, word_half in enumerate(word_halves):
+                nc.tensor.transpose(turned[:, u * P : (u + 1) * P], word_half, ident[:])
+            return turned
+
+        def unload(copy, words, turned):
+            copy(out=words.rearrange("p (c u) -> p c u", u=2), in_=turned[:, 0 : 2 * P].rearrange("p (u c) -> p c u", u=2))
 
         def value_halves(t):
             words = picked[t][:].bitcast(F32).rearrange("p (s u) -> p u s", u=2)
@@ -137,15 +139,27 @@ def tile_attend_gatedkeys_pl_kernel(tc, query, keys, kgate, size, vals, offs, ou
             nc.vector.quantize_mx(out=codes.bitcast(FP8X4), scales=scales, in_=words.bitcast(BF16))
             return [(codes[:, j * P : (j + 1) * P], scales[:, j * P : (j + 1) * P]) for j in range(n)]
 
+        v_turned = [turn(f"v{t}", value_halves(t)) for t in range(2)]
+
+        size_bank = bank("size_bank")
+        for t in range(PACK):
+            nc.tensor.transpose(size_bank[:].rearrange("p (u s r) -> p u r s", u=2, r=2)[:, t // 2, t % 2], size_cols[:, t : t + 1].to_broadcast([P, P]), ident[:])
+
+        neg_max = [sbuf(f"neg_max{b}", [P, 1], F32) for b in range(2)]
+        both_sums = sbuf("sums", [P, 2], F32, "val_pool1")
+        sums = [both_sums[:, b : b + 1] for b in range(2)]
+        inv = [sbuf(f"inv{b}", [P, 1], F32) for b in range(2)]
+        probs = [sbuf(f"probs{b}", [P, 2, P, 2], F32) for b in range(2)]
         for b in range(2):
-            nc.vector.tensor_reduce(neg_max[:, b : b + 1], scores[b][:], AX.X, ALU.max, negate=True)
+            nc.vector.tensor_reduce(neg_max[b][:], scores[b][:], AX.X, ALU.max, negate=True)
             nc.scalar.activation(probs[b][:], scores[b][:].rearrange("p (s u r) -> p u s r", u=2, r=2), ACT.Exp,
-                                 bias=neg_max[:, b : b + 1], accum_out=sums[b])
-        nc.vector.tensor_copy(picked[2][:], listed(val_pool[2], 0, I))
-        for b in range(2):
-            nc.vector.reciprocal(inv[b][:], sums[b])
-        v01_words = sbuf("v01_words", [P, 4 * P], F32)[:]
-        turn("v01", value_halves(0) + value_halves(1), v01_words, nc.scalar.copy)
+                                 bias=neg_max[b][:], accum_out=sums[b])
+        nc.vector.tensor_copy(picked[2][:, 0:SHARE2], listed(val_pool[2], 0, SHARE2))
+        nc.scalar.activation(picked[2][:, SHARE2:I], listed(val_pool[2], SHARE2, I), ACT.Copy)
+        v0_words = sbuf("v0_words", [P, 2 * P], F32, "neg_max0")[:]
+        nc.vector.reciprocal(inv[0][:], sums[0])
+        unload(nc.vector.tensor_copy, v0_words, v_turned[0])
+        nc.vector.reciprocal(inv[1][:], sums[1])
         nc.scalar.activation(picked[3][:], listed(val_pool[3], 0, I), ACT.Copy)
         w_bf = [sbuf(f"w_bf{b}", [P, 2, HALF], BF16) for b in range(2)]
         flat = [probs[b][:].rearrange("p u s r -> p u (s r)") for b in range(2)]
@@ -155,15 +169,21 @@ def tile_attend_gatedkeys_pl_kernel(tc, query, keys, kgate, size, vals, offs, ou
             nc.vector.scalar_tensor_tensor(w_bf[1][:, u], flat[1][:, u], inv[1][:], size_dealt[:, u], ALU.mult, ALU.mult)
 
         w_words = [sbuf(f"w{b}_words", [P, 2 * P], F32)[:] for b in range(2)]
-        v2_words, v3_words = sbuf("v2_words", [P, 2 * P], F32, "val_pool3")[:], sbuf("v3_words", [P, 2 * P], F32)[:]
-        turn("w0", [w_bf[0][:, u].bitcast(F32) for u in range(2)], w_words[0], nc.vector.tensor_copy, "scores0")
-        turn("v2", value_halves(2), v2_words, nc.scalar.copy, "v01_turned")
-        turn("w1", [w_bf[1][:, u].bitcast(F32) for u in range(2)], w_words[1], nc.scalar.copy, "scores1")
-        turn("v3", value_halves(3), v3_words, nc.scalar.copy)
-        v_mx = quantize_words("v01", v01_words, "probs0") + quantize_words("v2", v2_words)
-        w_mx = quantize_words("w0", w_words[0]) + quantize_words("w1", w_words[1])
+        v12_words, v3_words = sbuf("v12_words", [P, 4 * P], F32, "probs0")[:], sbuf("v3_words", [P, 2 * P], F32)[:]
+        v2_turned = turn("v2", value_halves(2), "v0_turned")
+        w0_turned = turn("w0", [w_bf[0][:, u].bitcast(F32) for u in range(2)], "scores0")
+        w1_turned = turn("w1", [w_bf[1][:, u].bitcast(F32) for u in range(2)], "scores1")
+        v3_turned = turn("v3", value_halves(3))
+        unload(nc.scalar.copy, v12_words[:, 0 : 2 * P], v_turned[1])
+        unload(nc.scalar.copy, w_words[0], w0_turned)
+        unload(nc.vector.tensor_copy, v12_words[:, 2 * P : 4 * P], v2_turned)
+        v_mx = quantize_words("v0", v0_words, "inv0")
+        v_mx = v_mx + quantize_words("v12", v12_words)
+        unload(nc.scalar.copy, w_words[1], w1_turned)
+        unload(nc.scalar.copy, v3_words, v3_turned)
+        w_mx = quantize_words("w0", w_words[0])
+        w_mx = w_mx + quantize_words("w1", w_words[1])
         v_mx = v_mx + quantize_words("v3", v3_words)
-
         o_codes = sbuf("o_codes", [P, Q], U32)
         o_scales = sbuf("o_scales", [P, Q], U8)
         out_rows = out_0.rearrange("(p t) q -> p t q", t=PACK)
@@ -181,15 +201,17 @@ def tile_attend_gatedkeys_pl_kernel(tc, query, keys, kgate, size, vals, offs, ou
             nc.sync.dma_start(out_rows[:, first:stop, :], result[:, first:stop, :])
 
         result_planes(0, 0, 3, None, nc.scalar.copy)
-        result_planes(1, 0, 3, None, nc.vector.tensor_copy)
+        result_planes(1, 0, 2, None, nc.vector.tensor_copy)
         store_planes(0, 2)
+        result_planes(1, 2, 3, "v1_turned", nc.scalar.copy)
         result_planes(0, 3, 4, "size_bank", nc.scalar.copy)
-        result_planes(1, 3, 4, None, nc.vector.tensor_copy)
+        result_planes(1, 3, 4, "scores0", nc.vector.tensor_copy)
         store_planes(2, 4)
 
-        for copy, cols in zip((nc.scalar.copy, nc.vector.tensor_copy), blocks):
+        quarters = [slice(j * P // 2, (j + 1) * P // 2) for j in range(4)]
+        for copy, cols in ((nc.vector.tensor_copy, blocks[0]), (nc.scalar.copy, quarters[2]), (nc.vector.tensor_copy, quarters[3])):
             weave(copy, result_bf[:, cols, :], result[:, :, cols])
-        for cols in reversed(blocks):
+        for cols in blocks:
             quantize(o_codes[:, cols], o_scales[:, cols], result_bf[:, cols, :])
         nc.sync.dma_start(out_words, o_codes[:].bitcast(I32))
         for g in range(4):

@@ -18,8 +18,7 @@ D, T, I, Q, E = 512, 1024, 512, 256, 512
 P = 128
 PACK = 4
 HALF = I // 2
-SHARE2 = 7 * I // 8
-SHARE = 3 * I // 4
+SHARE = 5 * I // 8
 LIST_ROWS = 16
 FLOPS = 2 * D * Q * I + 2 * I * E * Q
 
@@ -154,8 +153,7 @@ def tile_attend_gatedkeys_pl_kernel(tc, query, keys, kgate, size, vals, offs, ou
             nc.vector.tensor_reduce(neg_max[b][:], scores[b][:], AX.X, ALU.max, negate=True)
             nc.scalar.activation(probs[b][:], scores[b][:].rearrange("p (s u r) -> p u s r", u=2, r=2), ACT.Exp,
                                  bias=neg_max[b][:], accum_out=sums[b])
-        nc.vector.tensor_copy(picked[2][:, 0:SHARE2], listed(val_pool[2], 0, SHARE2))
-        nc.scalar.activation(picked[2][:, SHARE2:I], listed(val_pool[2], SHARE2, I), ACT.Copy)
+        nc.vector.tensor_copy(picked[2][:], listed(val_pool[2], 0, I))
         v0_words = sbuf("v0_words", [P, 2 * P], F32, "neg_max0")[:]
         nc.vector.reciprocal(inv[0][:], sums[0])
         unload(nc.vector.tensor_copy, v0_words, v_turned[0])

@@ -46,9 +46,8 @@ def tile_attend_gatedkeys_pl_kernel(tc, query, keys, kgate, size, vals, offs, ou
                                 rhs=moving[0].bitcast(FP8X4), rhs_scale=moving[1], start=True, stop=True)
 
         offsets = sbuf("offsets", [P, I // LIST_ROWS], U16)
-        gate_pair, key_pair = sbuf("gate_pair", [P, 2 * T], F32), sbuf("key_pair", [P, 2 * T], F32)
-        gate_pool = {t: sbuf(f"gate_pool{t}", [P, T], F32) for t in range(2, PACK)}
-        key_pool = {t: sbuf(f"key_pool{t}", [P, T], F32) for t in range(2, PACK)}
+        gate_pool = [sbuf(f"gate_pool{t}", [P, T], F32) for t in range(PACK)]
+        key_pool = [sbuf(f"key_pool{t}", [P, T], F32) for t in range(PACK)]
         val_pool = [sbuf(f"val_pool{t}", [P, T], F32) for t in range(PACK)]
         query_raw = sbuf("query_raw", [P, PACK, Q], F32)
         size_cols = sbuf("size_cols", [P, PACK], F32)
@@ -56,9 +55,11 @@ def tile_attend_gatedkeys_pl_kernel(tc, query, keys, kgate, size, vals, offs, ou
         def load_plane(pool, source, t):
             nc.sync.dma_start(pool[t][:], source.rearrange("(p t) n -> p t n", t=PACK)[:, t, :])
 
-        nc.sync.dma_start(gate_pair[:], kgate.rearrange("(p t) n -> p (t n)", t=PACK)[:, 0 : 2 * T])
+        load_plane(gate_pool, kgate, 0)
         nc.sync.dma_start(offsets[:], offs)
-        nc.sync.dma_start(key_pair[:], keys.rearrange("(p t) n -> p (t n)", t=PACK)[:, 0 : 2 * T])
+        load_plane(key_pool, keys, 0)
+        load_plane(gate_pool, kgate, 1)
+        load_plane(key_pool, keys, 1)
         for pool, source in ((gate_pool, kgate), (key_pool, keys)):
             for t in range(2, PACK):
                 load_plane(pool, source, t)
@@ -79,19 +80,12 @@ def tile_attend_gatedkeys_pl_kernel(tc, query, keys, kgate, size, vals, offs, ou
         halves = [slice(h * HALF, (h + 1) * HALF) for h in range(2)]
         quarter = [slice(j * I // 4, (j + 1) * I // 4) for j in range(4)]
         last_pieces = [quarter[0], slice(quarter[1].start, quarter[2].stop), quarter[3]]
-        gate1, key1 = sbuf("raw_gate1", [P, I], F32), sbuf("raw_key1", [P, I], F32)
-        nc.vector.tensor_copy(gate1[:], gate_pair[:, T : 2 * T].indirect(offsets[:]))
-        nc.scalar.activation(gates[0][:], listed(gate_pair, 0, I), ACT.Sigmoid)
-        nc.scalar.activation(gates[1][:], gate1[:], ACT.Sigmoid)
-        nc.vector.tensor_copy(key1[:], key_pair[:, T : 2 * T].indirect(offsets[:]))
-        nc.vector.tensor_tensor(km[:, 0], listed(key_pair, 0, I), gates[0][:], ALU.mult)
-        nc.vector.tensor_tensor(km[:, 1], key1[:], gates[1][:], ALU.mult)
-        for t in range(2, PACK):
+        for t in range(PACK):
             nc.scalar.activation(gates[t][:], listed(gate_pool[t], 0, I), ACT.Sigmoid)
             for cols in last_pieces if t == PACK - 1 else [slice(0, I)]:
                 nc.vector.tensor_tensor(km[:, t, cols], listed(key_pool[t], cols.start, cols.stop), gates[t][:, cols], ALU.mult)
         exp_warm = sbuf("exp_warm", [P, 1], F32)
-        nc.scalar.activation(exp_warm[:], gate_pool[PACK - 1][:, 0:1], ACT.Exp)
+        nc.scalar.activation(exp_warm[:], gates[PACK - 1][:, I - 1 : I], ACT.Exp)
 
         blocks = [slice(b * P, (b + 1) * P) for b in range(2)]
         km_bf = sbuf("km_bf", [P, I, PACK], BF16)
@@ -173,8 +167,8 @@ def tile_attend_gatedkeys_pl_kernel(tc, query, keys, kgate, size, vals, offs, ou
         w1_turned = turn("w1", [w_bf[1][:, u].bitcast(F32) for u in range(2)], "scores1")
         v3_turned = turn("v3", value_halves(3))
         unload(nc.scalar.copy, v12_words[:, 0 : 2 * P], v_turned[1])
+        unload(nc.scalar.copy, v12_words[:, 2 * P : 4 * P], v2_turned)
         unload(nc.scalar.copy, w_words[0], w0_turned)
-        unload(nc.vector.tensor_copy, v12_words[:, 2 * P : 4 * P], v2_turned)
         v_mx = quantize_words("v0", v0_words, "inv0")
         v_mx = v_mx + quantize_words("v12", v12_words)
         unload(nc.scalar.copy, w_words[1], w1_turned)
@@ -203,7 +197,7 @@ def tile_attend_gatedkeys_pl_kernel(tc, query, keys, kgate, size, vals, offs, ou
         store_planes(0, 2)
         result_planes(1, 2, 3, "v1_turned", nc.scalar.copy)
         result_planes(0, 3, 4, "size_bank", nc.scalar.copy)
-        result_planes(1, 3, 4, "scores0", nc.vector.tensor_copy)
+        result_planes(1, 3, 4, "scores0", nc.scalar.copy)
         store_planes(2, 4)
 
         quarters = [slice(j * P // 2, (j + 1) * P // 2) for j in range(4)]

@@ -18,7 +18,8 @@ D, T, I, Q, E = 512, 1024, 512, 256, 512
 P = 128
 PACK = 4
 HALF = I // 2
-SHARE = 5 * I // 8
+FUSED = 7 * I // 16
+SHARE = I // 2
 LIST_ROWS = 16
 FLOPS = 2 * D * Q * I + 2 * I * E * Q
 
@@ -57,18 +58,18 @@ def tile_attend_gatedkeys_pl_kernel(tc, query, keys, kgate, size, vals, offs, ou
 
         load_plane(gate_pool, kgate, 0)
         nc.sync.dma_start(offsets[:], offs)
-        load_plane(key_pool, keys, 0)
-        load_plane(gate_pool, kgate, 1)
-        load_plane(key_pool, keys, 1)
-        for pool, source in ((gate_pool, kgate), (key_pool, keys)):
-            for t in range(2, PACK):
-                load_plane(pool, source, t)
+        for t in range(1, PACK):
+            load_plane(gate_pool, kgate, t)
+        for t in range(PACK):
+            load_plane(key_pool, keys, t)
         nc.sync.dma_start(query_raw[:], query.rearrange("(p t) q -> p t q", t=PACK))
         for t in range(PACK - 1):
             load_plane(val_pool, vals, t)
         nc.sync.dma_start(size_cols[:], size.rearrange("o (p t) -> p (o t)", t=PACK))
         load_plane(val_pool, vals, PACK - 1)
 
+        warm_zero = sbuf("warm_zero", [P, 1], F32)
+        nc.gpsimd.memset(warm_zero[:], 0.0)
         ident = sbuf("ident", [P, P], F32)
         make_identity(nc, ident[:])
 
@@ -78,33 +79,41 @@ def tile_attend_gatedkeys_pl_kernel(tc, query, keys, kgate, size, vals, offs, ou
         gates = [sbuf(f"gate{t}", [P, I], F32) for t in range(PACK)]
         km = sbuf("km", [P, PACK, I], F32)
         halves = [slice(h * HALF, (h + 1) * HALF) for h in range(2)]
-        quarter = [slice(j * I // 4, (j + 1) * I // 4) for j in range(4)]
-        last_pieces = [quarter[0], slice(quarter[1].start, quarter[2].stop), quarter[3]]
+        last_pieces = [slice(0, FUSED), slice(FUSED, 3 * I // 4), slice(3 * I // 4, I)]
+        sigmoid_warm = sbuf("sigmoid_warm", [P, 1], F32)
+        nc.scalar.activation(sigmoid_warm[:], warm_zero[:], ACT.Sigmoid)
         for t in range(PACK):
-            nc.scalar.activation(gates[t][:], listed(gate_pool[t], 0, I), ACT.Sigmoid)
-            for cols in last_pieces if t == PACK - 1 else [slice(0, I)]:
-                nc.vector.tensor_tensor(km[:, t, cols], listed(key_pool[t], cols.start, cols.stop), gates[t][:, cols], ALU.mult)
+            for cols in halves if t == PACK - 1 else [slice(0, I)]:
+                nc.scalar.activation(gates[t][:, cols], listed(gate_pool[t], cols.start, cols.stop), ACT.Sigmoid)
         exp_warm = sbuf("exp_warm", [P, 1], F32)
-        nc.scalar.activation(exp_warm[:], gates[PACK - 1][:, I - 1 : I], ACT.Exp)
+        nc.scalar.activation(exp_warm[:], gates[PACK - 1][:, 0:1], ACT.Exp)
+
+        for t, fused, split in ((0, [slice(0, I)], []), (1, [slice(0, I)], []), (2, halves[0:1], halves[1:2]), (3, last_pieces[0:1], last_pieces[1:3])):
+            raw = sbuf(f"raw_key{t}", [P, I], F32) if split else None
+            for cols in split:
+                nc.scalar.activation(raw[:, cols], listed(key_pool[t], cols.start, cols.stop), ACT.Copy)
+            for cols in fused:
+                nc.vector.tensor_tensor(km[:, t, cols], listed(key_pool[t], cols.start, cols.stop), gates[t][:, cols], ALU.mult)
+            for cols in split:
+                nc.vector.tensor_tensor(km[:, t, cols], raw[:, cols], gates[t][:, cols], ALU.mult)
 
         blocks = [slice(b * P, (b + 1) * P) for b in range(2)]
         km_bf = sbuf("km_bf", [P, I, PACK], BF16)
         q_bf = sbuf("q_bf", [P, Q, PACK], BF16)
         q_codes, q_scales = sbuf("q_codes", [P, Q], U32), sbuf("q_scales", [P, Q], U8)
         k_codes, k_scales = sbuf("k_codes", [P, I], U32), sbuf("k_scales", [P, I], U8)
-        for cols in quarter[0:2]:
-            weave(nc.scalar.copy, km_bf[:, cols, :], km[:, :, cols])
-        for cols in quarter[2:4]:
+        weave(nc.scalar.copy, km_bf[:, last_pieces[0], :], km[:, :, last_pieces[0]])
+        for cols in last_pieces[1:3]:
             weave(nc.vector.tensor_copy, km_bf[:, cols, :], km[:, :, cols])
         weave(nc.vector.tensor_copy, q_bf[:, blocks[0], :], query_raw[:, :, blocks[0]])
         weave(nc.scalar.copy, q_bf[:, blocks[1], :], query_raw[:, :, blocks[1]])
         for b in range(2):
-            quantize(k_codes[:, halves[b]], k_scales[:, halves[b]], km_bf[:, halves[b], :])
+            quantize(k_codes[:, halves[1 - b]], k_scales[:, halves[1 - b]], km_bf[:, halves[1 - b], :])
             quantize(q_codes[:, blocks[b]], q_scales[:, blocks[b]], q_bf[:, blocks[b], :])
 
         scores = [bank(f"scores{b}") for b in range(2)]
         for b in range(2):
-            for cols in halves:
+            for cols in reversed(halves):
                 product(scores[b][:, cols], (q_codes[:, blocks[b]], q_scales[:, blocks[b]]), (k_codes[:, cols], k_scales[:, cols]))
 
         picked = [sbuf(f"picked{t}", [P, I], BF16) for t in range(PACK)]

from contextlib import ExitStack

import concourse.mybir as mybir
from concourse.masks import make_identity

F32 = mybir.dt.float32
BF16 = mybir.dt.bfloat16
I32 = mybir.dt.int32
U32 = mybir.dt.uint32
U16 = mybir.dt.uint16
U8 = mybir.dt.uint8
FP8X4 = mybir.dt.float8_e4m3fn_x4
ACT = mybir.ActivationFunctionType
ALU = mybir.AluOpType
AX = mybir.AxisListType

D, T, I, Q, E = 512, 1024, 512, 256, 512
P = 128
PACK = 4
HALF = I // 2
FUSED = 7 * I // 16
SHARE = I // 2
LIST_ROWS = 16
FLOPS = 2 * D * Q * I + 2 * I * E * Q


def tile_attend_gatedkeys_pl_kernel(tc, query, keys, kgate, size, vals, offs, out_0, out_1, out_2):
    nc = tc.nc
    with ExitStack() as ctx:
        sb = ctx.enter_context(tc.tile_pool(name="sb", bufs=1))
        ps = ctx.enter_context(tc.psum_pool(name="ps", bufs=1))

        def sbuf(name, shape, dtype, bytes_of=None):
            return sb.tile(shape, dtype, name=name, tag=bytes_of or name, align_bytes=64)

        def bank(name, bytes_of=None):
            return ps.tile([P, 512], F32, name=name, tag=bytes_of or name)

        def weave(copy, dst, src):
            copy(out=dst.rearrange("p (c i) t -> p c t i", i=4), in_=src.rearrange("p t (c i) -> p c t i", i=4))

        def quantize(codes, scales, woven):
            nc.vector.quantize_mx(out=codes.bitcast(FP8X4), scales=scales, in_=woven.rearrange("p c t -> p (c t)"))

        def product(out, stationary, moving):
            nc.tensor.matmul_mx(out=out, lhsT=stationary[0].bitcast(FP8X4), lhsT_scale=stationary[1],
                                rhs=moving[0].bitcast(FP8X4), rhs_scale=moving[1], start=True, stop=True)

        offsets = sbuf("offsets", [P, I // LIST_ROWS], U16)
        gate_pool = [sbuf(f"gate_pool{t}", [P, T], F32) for t in range(PACK)]
        key_pool = [sbuf(f"key_pool{t}", [P, T], F32) for t in range(PACK)]
        val_pool = [sbuf(f"val_pool{t}", [P, T], F32) for t in range(PACK)]
        query_raw = sbuf("query_raw", [P, PACK, Q], F32)
        size_cols = sbuf("size_cols", [P, PACK], F32)

        def load_plane(pool, source, t):
            nc.sync.dma_start(pool[t][:], source.rearrange("(p t) n -> p t n", t=PACK)[:, t, :])

        load_plane(gate_pool, kgate, 0)
        nc.sync.dma_start(offsets[:], offs)
        for t in range(1, PACK):
            load_plane(gate_pool, kgate, t)
        for t in range(PACK):
            load_plane(key_pool, keys, t)
        nc.sync.dma_start(query_raw[:], query.rearrange("(p t) q -> p t q", t=PACK))
        for t in range(PACK - 1):
            load_plane(val_pool, vals, t)
        nc.sync.dma_start(size_cols[:], size.rearrange("o (p t) -> p (o t)", t=PACK))
        load_plane(val_pool, vals, PACK - 1)

        warm_zero = sbuf("warm_zero", [P, 1], F32)
        nc.gpsimd.memset(warm_zero[:], 0.0)
        ident = sbuf("ident", [P, P], F32)
        make_identity(nc, ident[:])

        def listed(pool_tile, start, stop):
            return pool_tile[:].indirect(offsets[:, start // LIST_ROWS : stop // LIST_ROWS])

        gates = [sbuf(f"gate{t}", [P, I], F32) for t in range(PACK)]
        km = sbuf("km", [P, PACK, I], F32)
        halves = [slice(h * HALF, (h + 1) * HALF) for h in range(2)]
        last_pieces = [slice(0, FUSED), slice(FUSED, 3 * I // 4), slice(3 * I // 4, I)]
        sigmoid_warm = sbuf("sigmoid_warm", [P, 1], F32)
        nc.scalar.activation(sigmoid_warm[:], warm_zero[:], ACT.Sigmoid)
        for t in range(PACK):
            for cols in halves if t == PACK - 1 else [slice(0, I)]:
                nc.scalar.activation(gates[t][:, cols], listed(gate_pool[t], cols.start, cols.stop), ACT.Sigmoid)
        exp_warm = sbuf("exp_warm", [P, 1], F32)
        nc.scalar.activation(exp_warm[:], gates[PACK - 1][:, 0:1], ACT.Exp)

        for t, fused, split in ((0, [slice(0, I)], []), (1, [slice(0, I)], []), (2, halves[0:1], halves[1:2]), (3, last_pieces[0:1], last_pieces[1:3])):
            raw = sbuf(f"raw_key{t}", [P, I], F32) if split else None
            for cols in split:
                nc.scalar.activation(raw[:, cols], listed(key_pool[t], cols.start, cols.stop), ACT.Copy)
            for cols in fused:
                nc.vector.tensor_tensor(km[:, t, cols], listed(key_pool[t], cols.start, cols.stop), gates[t][:, cols], ALU.mult)
            for cols in split:
                nc.vector.tensor_tensor(km[:, t, cols], raw[:, cols], gates[t][:, cols], ALU.mult)

        blocks = [slice(b * P, (b + 1) * P) for b in range(2)]
        km_bf = sbuf("km_bf", [P, I, PACK], BF16)
        q_bf = sbuf("q_bf", [P, Q, PACK], BF16)
        q_codes, q_scales = sbuf("q_codes", [P, Q], U32), sbuf("q_scales", [P, Q], U8)
        k_codes, k_scales = sbuf("k_codes", [P, I], U32), sbuf("k_scales", [P, I], U8)
        weave(nc.scalar.copy, km_bf[:, last_pieces[0], :], km[:, :, last_pieces[0]])
        for cols in last_pieces[1:3]:
            weave(nc.vector.tensor_copy, km_bf[:, cols, :], km[:, :, cols])
        weave(nc.vector.tensor_copy, q_bf[:, blocks[0], :], query_raw[:, :, blocks[0]])
        weave(nc.scalar.copy, q_bf[:, blocks[1], :], query_raw[:, :, blocks[1]])
        for b in range(2):
            quantize(k_codes[:, halves[1 - b]], k_scales[:, halves[1 - b]], km_bf[:, halves[1 - b], :])
            quantize(q_codes[:, blocks[b]], q_scales[:, blocks[b]], q_bf[:, blocks[b], :])

        scores = [bank(f"scores{b}") for b in range(2)]
        for b in range(2):
            for cols in reversed(halves):
                product(scores[b][:, cols], (q_codes[:, blocks[b]], q_scales[:, blocks[b]]), (k_codes[:, cols], k_scales[:, cols]))

        picked = [sbuf(f"picked{t}", [P, I], BF16) for t in range(PACK)]
        nc.scalar.activation(picked[0][:, 0:SHARE], listed(val_pool[0], 0, SHARE), ACT.Copy)
        nc.vector.tensor_copy(picked[0][:, SHARE:I], listed(val_pool[0], SHARE, I))
        for cols in halves:
            nc.scalar.activation(picked[1][:, cols], listed(val_pool[1], cols.start, cols.stop), ACT.Copy)

        def turn(name, word_halves, bank_of=None):
            turned = bank(name + "_turned", bank_of)
            for u, word_half in enumerate(word_halves):
                nc.tensor.transpose(turned[:, u * P : (u + 1) * P], word_half, ident[:])
            return turned

        def unload(copy, words, turned):
            copy(out=words.rearrange("p (c u) -> p c u", u=2), in_=turned[:, 0 : 2 * P].rearrange("p (u c) -> p c u", u=2))

        def value_halves(t):
            words = picked[t][:].bitcast(F32).rearrange("p (s u) -> p u s", u=2)
            return [words[:, u] for u in range(2)]

        def quantize_words(name, words, scales_of=None):
            n = words.shape[1] // (2 * P)
            codes, scales = sbuf(name + "_codes", [P, n * P], U32)[:], sbuf(name + "_scales", [P, n * P], U8, scales_of)[:]
            nc.vector.quantize_mx(out=codes.bitcast(FP8X4), scales=scales, in_=words.bitcast(BF16))
            return [(codes[:, j * P : (j + 1) * P], scales[:, j * P : (j + 1) * P]) for j in range(n)]

        v_turned = [turn(f"v{t}", value_halves(t)) for t in range(2)]

        size_bank = bank("size_bank")
        for t in range(PACK):
            nc.tensor.transpose(size_bank[:].rearrange("p (u s r) -> p u r s", u=2, r=2)[:, t // 2, t % 2], size_cols[:, t : t + 1].to_broadcast([P, P]), ident[:])

        neg_max = [sbuf(f"neg_max{b}", [P, 1], F32) for b in range(2)]
        both_sums = sbuf("sums", [P, 2], F32, "val_pool1")
        sums = [both_sums[:, b : b + 1] for b in range(2)]
        inv = [sbuf(f"inv{b}", [P, 1], F32) for b in range(2)]
        probs = [sbuf(f"probs{b}", [P, 2, P, 2], F32) for b in range(2)]
        for b in range(2):
            nc.vector.tensor_reduce(neg_max[b][:], scores[b][:], AX.X, ALU.max, negate=True)
            nc.scalar.activation(probs[b][:], scores[b][:].rearrange("p (s u r) -> p u s r", u=2, r=2), ACT.Exp,
                                 bias=neg_max[b][:], accum_out=sums[b])
        nc.vector.tensor_copy(picked[2][:], listed(val_pool[2], 0, I))
        v0_words = sbuf("v0_words", [P, 2 * P], F32, "neg_max0")[:]
        nc.vector.reciprocal(inv[0][:], sums[0])
        unload(nc.vector.tensor_copy, v0_words, v_turned[0])
        nc.vector.reciprocal(inv[1][:], sums[1])
        nc.scalar.activation(picked[3][:], listed(val_pool[3], 0, I), ACT.Copy)
        w_bf = [sbuf(f"w_bf{b}", [P, 2, HALF], BF16) for b in range(2)]
        flat = [probs[b][:].rearrange("p u s r -> p u (s r)") for b in range(2)]
        size_dealt = size_bank[:].rearrange("p (u c) -> p u c", u=2)
        nc.vector.scalar_tensor_tensor(w_bf[0][:], flat[0], inv[0][:], size_dealt, ALU.mult, ALU.mult)
        for u in range(2):
            nc.vector.scalar_tensor_tensor(w_bf[1][:, u], flat[1][:, u], inv[1][:], size_dealt[:, u], ALU.mult, ALU.mult)

        w_words = [sbuf(f"w{b}_words", [P, 2 * P], F32)[:] for b in range(2)]
        v12_words, v3_words = sbuf("v12_words", [P, 4 * P], F32, "probs0")[:], sbuf("v3_words", [P, 2 * P], F32)[:]
        v2_turned = turn("v2", value_halves(2), "v0_turned")
        w0_turned = turn("w0", [w_bf[0][:, u].bitcast(F32) for u in range(2)], "scores0")
        w1_turned = turn("w1", [w_bf[1][:, u].bitcast(F32) for u in range(2)], "scores1")
        v3_turned = turn("v3", value_halves(3))
        unload(nc.scalar.copy, v12_words[:, 0 : 2 * P], v_turned[1])
        unload(nc.scalar.copy, v12_words[:, 2 * P : 4 * P], v2_turned)
        unload(nc.scalar.copy, w_words[0], w0_turned)
        v_mx = quantize_words("v0", v0_words, "inv0")
        v_mx = v_mx + quantize_words("v12", v12_words)
        unload(nc.scalar.copy, w_words[1], w1_turned)
        unload(nc.scalar.copy, v3_words, v3_turned)
        w_mx = quantize_words("w0", w_words[0])
        w_mx = w_mx + quantize_words("w1", w_words[1])
        v_mx = v_mx + quantize_words("v3", v3_words)
        o_codes = sbuf("o_codes", [P, Q], U32)
        o_scales = sbuf("o_scales", [P, Q], U8)
        out_rows = out_0.rearrange("(p t) q -> p t q", t=PACK)
        out_words = out_1.rearrange("z p c r -> p (z c r)").bitcast(I32)
        result = sbuf("result", [P, PACK, Q], F32)
        result_bf = sbuf("result_bf", [P, Q, PACK], BF16)

        def result_planes(b, first, stop, bank_of, copy):
            acc = bank(f"acc{b}_{first}", bank_of)
            for t in range(first, stop):
                product(acc[:, (t - first) * P : (t - first + 1) * P], v_mx[t], w_mx[b])
            copy(out=result[:, first:stop, b * P : (b + 1) * P], in_=acc[:, 0 : (stop - first) * P].rearrange("p (t q) -> p t q", q=P))

        def store_planes(first, stop):
            nc.sync.dma_start(out_rows[:, first:stop, :], result[:, first:stop, :])

        result_planes(0, 0, 3, None, nc.scalar.copy)
        result_planes(1, 0, 2, None, nc.vector.tensor_copy)
        store_planes(0, 2)
        result_planes(1, 2, 3, "v1_turned", nc.scalar.copy)
        result_planes(0, 3, 4, "size_bank", nc.scalar.copy)
        result_planes(1, 3, 4, "scores0", nc.scalar.copy)
        store_planes(2, 4)

        quarters = [slice(j * P // 2, (j + 1) * P // 2) for j in range(4)]
        for copy, cols in ((nc.vector.tensor_copy, blocks[0]), (nc.scalar.copy, quarters[2]), (nc.vector.tensor_copy, quarters[3])):
            weave(copy, result_bf[:, cols, :], result[:, :, cols])
        for cols in blocks:
            quantize(o_codes[:, cols], o_scales[:, cols], result_bf[:, cols, :])
        nc.sync.dma_start(out_words, o_codes[:].bitcast(I32))
        for g in range(4):
            queue = nc.sync if g % 2 == 0 else nc.scalar
            queue.dma_start(out_2[0, 4 * g : 4 * g + 4, :].bitcast(I32), o_scales[32 * g : 32 * g + 4, :].bitcast(I32))
